import numpy as np, ml_dtypes
CORES = [2,3,42,43,82,83,122,123]
N = 8
import mx_ref
BF = ml_dtypes.bfloat16
def gentries(a):
    return np.ascontiguousarray(a.reshape(8, 16, -1).transpose(0, 2, 1)).reshape(8, -1)
def gtable(e):
    e = np.asarray(e); return np.ascontiguousarray(e.reshape(8, -1, 16).transpose(0, 2, 1)).reshape(128, -1).astype(np.int32)
def gcols(t, e):
    v = np.concatenate([t.reshape(8, 16, -1, 4), np.zeros((8, 16, 1, 4), BF)], axis=2)
    return np.ascontiguousarray(np.stack([v[g][:, e[g]] for g in range(8)])).reshape(128, -1)
def gpick(z, e):
    return np.concatenate([z[16 * g:16 * g + 16][:, e[g]] for g in range(8)])
def tile(rs):
    return np.stack(rs, axis=2).reshape(128, -1).astype(BF)
def pick(q, e):
    c = np.concatenate([q[0].reshape(128, -1, 4), np.zeros((128, 1, 4), np.uint8)], axis=1); s = np.concatenate([q[1], np.ones((16, 1), np.uint8)], axis=1)
    return (np.ascontiguousarray(c[:, e].reshape(128, -1)), np.ascontiguousarray(s[:, e]))
def join(*qs):
    return (np.concatenate([q[0] for q in qs], axis=1), np.concatenate([q[1] for q in qs], axis=1))
def put(q, e, v):
    c, s = q[0].reshape(128, -1, 4).copy(), q[1].copy(); c[:, e] = v[0].reshape(128, -1, 4); s[:, e] = v[1]
    return (c.reshape(128, -1), s)
def pk(c, s):
    return (np.ascontiguousarray(c), mx_ref.live(s))
def emit(q):
    return q[0], q[1]
def packed(v, rng):
    q = [mx_ref.quantize(np.ascontiguousarray(v[r])) for r in range(N)]
    return np.stack([a for a, b in q]), np.stack([mx_ref.plane(b, rng) for a, b in q])
def values_of_codes():
    e, c = np.zeros((128, 128, 4), np.float32), np.zeros((128, 2, 4), np.uint8)
    e[np.arange(128), np.arange(128), 0] = 1
    c[:127, :, 0] = np.arange(256).reshape(2, 128).T[:127]
    return mx_ref.matmul(mx_ref.quantize(e.reshape(128, 512).astype(BF)), (c.reshape(128, 8), np.full((16, 2), 127, np.uint8))).T.reshape(-1).astype(np.float64)
CODE_VALUE, SCALE_VALUE = values_of_codes(), 2.0 ** (np.arange(256) - 127.0)
def decode(q):
    return (CODE_VALUE[q[0]].reshape(16, 8, -1, 4) * SCALE_VALUE[q[1]][:, None, :, None] + 0.0).reshape(128, -1).astype(np.float32)
def f(rng, *shape):
    return mx_ref.flush((rng.standard_normal(shape, dtype=np.float32) * np.exp2(rng.integers(-2, 3, shape[:-1] + (1,)))).astype(BF))
def wide(rng, *shape, cols=0):
    v = rng.standard_normal(shape, dtype=np.float32) * np.exp2(rng.integers(-12, 13, shape)).astype(np.float32)
    if cols: v *= np.repeat(np.exp2(rng.integers(-cols, cols + 1, shape[:-2] + (1, shape[-1] // 4))) * (rng.random(shape[:-2] + (1, shape[-1] // 4)) > 0.0625), 4, axis=-1).astype(np.float32)
    return mx_ref.flush(v.astype(BF))
C, H = 320, 160
STEP = [1, 2, 4]
G, OWN = np.arange(8)[:, None], np.tile(np.arange(C), (8, 1))
def numbers_of(rng):
    return {"x": np.array(f(rng, N, 128, 4 * C)), "u": np.array(f(rng, N, 128, 512)), "v": np.array(f(rng, N, 128, 512))}
def stored(a, m):
    return {"fl": np.stack([gtable(a[r]) for r in range(N)]), "ml": np.stack([gtable(m[r]) for r in range(N)])}
def pairs(o):
    m = np.zeros(o.shape, np.int64)
    np.put_along_axis(m, o[..., ::2], o[..., 1::2], axis=-1)
    np.put_along_axis(m, o[..., 1::2], o[..., ::2], axis=-1)
    return m
def ring(o):
    a = np.zeros(C, np.int64)
    a[o] = np.roll(o, -1)
    return a
def lists(rng):
    e = np.tile(np.arange(C), (N, 8, 1))
    return rng.permuted(e, axis=2), pairs(rng.permuted(e, axis=2))
def layers(rng, still=[]):
    w = np.array(f(rng, N, 128, 2048)).reshape(N, 8, 16, 4, 8, 16, 4)
    for i in still:
        w[:, :, i] = 0
        w[:, :, :, :, :, i] = 0
    return w
def weights(rng, w):
    c, s = packed(np.ascontiguousarray(w).reshape(N, 128, 2048), rng)
    return {"wc": c, "ws": s}
def parity():
    i = np.arange(N)
    return (i ^ (i >> 1) ^ (i >> 2)) % 2
def setup_inputs(rng):
    return {**numbers_of(rng), **stored(*lists(rng)), **weights(rng, layers(rng))}
def setup_inputs_ties(rng):
    d = numbers_of(rng)
    o = rng.permutation(N)
    k = rng.integers(0, 4, (N, 8, C))
    k[o[1]] += 1
    k[o[2], rng.permutation(8)[:4]] = 1
    a, m = lists(rng)
    g = int(rng.integers(8))
    a[:, g] = np.arange(C)
    m[:, g] = (np.arange(C) + H) % C
    k[o[3], g] = np.arange(C) >= H
    x = d["x"].reshape(N, 8, 16, C, 4)
    x[:, :, 0] = 0
    x[:, :, 0, :, 0] = k.astype(np.float32).astype(BF)
    u = d["u"].reshape(N, 128, 128, 4)
    u[:, :, ::16] = 0
    for r in range(N):
        for h in range(0, 128, 16): u[r, h, h, 0] = 0.0 if r == o[0] else -1.0 if r == o[1] else 1.0
    return {"x": x.reshape(N, 128, 4 * C), "u": u.reshape(N, 128, 512), "v": d["v"], **stored(a, m), **weights(rng, layers(rng, [0]))}
def setup_inputs_near(rng):
    d = numbers_of(rng)
    x = d["x"].astype(np.float32).reshape(N, 8, 16, C, 4)
    x[:, :, 0] = 0
    x[:, :, 8:] = 0
    x[:, :, 15, :, 0] = 2.0 ** -26
    u = d["u"].reshape(N, 128, 128, 4)
    u[:, :, ::16] = 0
    o = rng.permutation(N) % 4
    for r in range(N):
        c = rng.choice([-1.0, 1.0], (8, 1))
        s = rng.integers(0, 16, (8, C))
        digits = ((s[:, :, None] >> np.arange(4)) & 1) * np.exp2(np.arange(4) - 23.0)
        if o[r] < 2:
            x[r, :, 0, :, 0] = c
            x[r, :, 8] = digits
            x[r, :, 11, :, 0] = 2.0 ** -10
        elif o[r] == 2: x[r, :, 8] = digits * rng.choice([-1.0, 1.0], (8, C, 1))
        else:
            x[r, :, 8, :, 0] = np.where(s < 8, 1.25, 0.0) * 2.0 ** -30 * c
            x[r, :, 9, :, 0] = np.where(s < 8, 0.0, 1.125) * 2.0 ** -30 * c
            for g in rng.permutation(8)[:4]:
                e = rng.choice([-1.0, 1.0], C) * 2.0 ** -30
                x[r, g, 8, :, 0] = 1.25 * e
                x[r, g, 9, :, 0] = -1.125 * e
            x[r, :, 13, :, 0] = rng.choice([-1.0, 1.0], (8, C)) * 2.0 ** -30
        at = [0, C - 1, int(rng.integers(C)), int(rng.integers(C))]
        for g, j in zip(rng.permutation(8)[:4], at): x[r, g, 0, j, 0] = 2.0 ** 29 * rng.choice([-1.0, 1.0])
        k = 1.0 if o[r] == 0 else 2.0 ** -30
        for h in range(0, 128, 16):
            u[r, h, h, 0] = k if o[r] < 2 else 1.0
            if o[r] < 2: u[r, h + 11, h, 0] = k
            if o[r] < 3: u[r, h + 8, h] = k
            else:
                u[r, h + 8, h, 0] = k
                u[r, h + 9, h, 0] = 1.125 * k
                u[r, h + 14, h, 0] = k
    w = layers(rng, [0, 8, 9, 10, 11, 12, 13, 14, 15])
    for g in range(8): w[:, g, 13, 0, g, 14, 0] = 2.0 ** -5
    return {"x": x.reshape(N, 128, 4 * C).astype(BF), "u": u.reshape(N, 128, 512), "v": d["v"], **stored(*lists(rng)), **weights(rng, w)}
def setup_inputs_odd(rng):
    d = numbers_of(rng)
    x = (1.0 + (2 * rng.integers(0, 64, (N, 16, 8, C, 4)) + 1) * 2.0 ** -7) * np.exp2(-rng.integers(0, 7, (N, 16, 8, C, 4)).astype(np.float64)) * rng.choice([-1.0, 1.0], (N, 16, 8, C, 4))
    x[:, :, 0, :, 0] = (np.where((parity()[:, None] + np.arange(16)) % 2 == 0, 1.96875, 1.875) * 2.0 ** 8)[:, :, None]
    x[:, :, 1, :, 0] = rng.integers(8, 16, (N, 16, C)) * 2.0 ** -8
    u = d["u"].reshape(N, 16, 8, 128, 4)
    u[:, :, 0, ::16] = 0
    for r in range(N):
        for g in rng.permutation(8)[:2]:
            u[r, :, :, 16 * g] = 0
            u[r, 2 * g + parity()[r], 1, 16 * g, 0] = 1.0
    w = layers(rng, [0, 1, 8, 9])
    for g in range(8):
        for i in (0, 8): w[:, g, i, 0, g, i, 0] = -0.5
    return {"x": x.astype(np.float32).reshape(N, 128, 4 * C).astype(BF), "u": u.reshape(N, 128, 512), "v": d["v"], **stored(*lists(rng)), **weights(rng, w)}
def setup_inputs_ends(rng):
    d = numbers_of(rng)
    r0 = int(rng.integers(N))
    a = rng.permutation(np.array([r0, r0 ^ STEP[0], r0 ^ STEP[1], r0 ^ STEP[0] ^ STEP[1]]))
    z = rng.permutation(np.setdiff1d(np.arange(N), a))
    x = np.where(rng.random((N, 128, C, 4)) < 0.5, -1.0, -0.9375) * 2.0 ** 30
    x[:, 5] *= 2.0 ** -10
    c = rng.choice([-1.0, 1.0], (128, 1, 4))
    for r in z[:2]: x[r] = c * (1.0 + 0.125 * rng.integers(0, 8, (128, C, 4))) * 2.0 ** -30
    for r in z[2:]: x[r] = x[r] * rng.choice([-1.0, 1.0], (1, C, 1))
    size = np.full(N, 2.0 ** 30)
    size[a[2:]] = 2.0 ** -30
    size[z[1::2]] = 2.0 ** -30
    u = d["u"].astype(np.float32).reshape(N, 128, 128, 4)
    w = np.zeros((N, 128, 4, 128, 4), np.float32)
    i = np.arange(128)
    for b in range(4): w[:, i, b, i, b] = 32.0
    w[a[2], 5, 0, 5, 0] = 2.0 ** 8
    w[a[2], 6, 0, 6, 0] = 2.0 ** -8
    k = np.array([[0, 0, 2, 2, 1, 1, 3, 3], [2, 1, 0, 3, 0, 3, 2, 1]])[parity()][:, rng.permutation(8)]
    e, m = lists(rng)
    j = np.arange(C)
    for r in range(N):
        h = rng.permutation(8)
        u[r, :, ::16] = (np.where(h < 2, 0.0, h % 2 * 2.0 - 1.0) * size[r])[None, :, None]
        for g in range(8):
            t = int(rng.integers(4))
            if t: m[r, g] = [C - 1 - j, j ^ 1, (j + H) % C][t - 1]
            e[r, g] = [ring(rng.permutation(C)), j, ring(j), m[r, g]][k[r, g]]
    u[:, 5, ::16] = 0
    v = rng.choice([-1.0, 1.0], (N, 128, 512)) * size[:, None, None]
    return {"x": x.astype(np.float32).reshape(N, 128, 4 * C).astype(BF), "u": u.reshape(N, 128, 512).astype(BF), "v": v.astype(np.float32).astype(BF), **stored(e, m), **weights(rng, w.astype(BF))}
def setup_inputs_spread(rng):
    d = setup_inputs(rng)
    d["x"] = wide(rng, N, 128, 4 * C, cols=6)
    return d
def check_inputs(d):
    b = []
    for k in ("x", "u", "v"):
        a = np.abs(d[k].astype(np.float32))
        if not (np.isfinite(a).all() and ((a == 0) | (a >= 2.0 ** -30) & (a <= 2.0 ** 30)).all()): b.append("a value of " + k)
    none, least, most = [emit(mx_ref.quantize(np.full((128, 16), k, np.float32).astype(BF)))[1][0, 0] for k in (0.0, 2.0 ** -8, 2.0 ** 8)]
    for r in range(N):
        if (np.sort(gentries(d["fl"][r]), axis=1) != OWN).any(): b.append("fl: a group that doesn't name every column once")
        m = gentries(d["ml"][r])
        if ((m < 0) | (m >= C)).any() or (m == OWN).any() or (m[G, m] != OWN).any(): b.append("ml: columns that aren't each other's mates")
        if ((d["wc"][r] == 0x7F) | (d["wc"][r] == 0xFF)).any(): b.append("wc: a code that is no number")
        s = mx_ref.live(d["ws"][r])
        if ((s != none) & ((s < least) | (s > most))).any(): b.append("ws: a scale out of range")
    return b
def leaders(a, s):
    best, w = OWN, a
    for _ in range(C - 1):
        p, o = s[G, w], s[G, best]
        best = np.where((p > o) | (p == o) & (w < best), w, best)
        w = a[G, w]
    return best
def hops(a, best):
    n, w = np.zeros((8, C), np.int64), best
    for _ in range(C - 1):
        go = w != OWN
        n, w = n + go, np.where(go, a[G, w], w)
    return n
def walk(a, at, n):
    for i in range(C - 1): at = np.where(i < n, a[G, at], at)
    return at
def reference(x, u, v, fl, ml, wc, ws):
    qu = [mx_ref.quantize(u[r]) for r in range(N)]
    lay = [pk(wc[r], ws[r]) for r in range(N)]
    cyc, mate = [gentries(fl[r]) for r in range(N)], [gentries(ml[r]) for r in range(N)]
    now = [x[r] for r in range(N)]
    for step in STEP:
        q = [mx_ref.quantize(now[r]) for r in range(N)]
        t = [decode(q[r]).astype(BF) for r in range(N)]
        made, after = [], []
        for r in range(N):
            p = r ^ step
            s = mx_ref.matmul(qu[r], q[r])[::16] + np.float32(0.0)
            lead = leaders(cyc[r], s)
            far = walk(cyc[p], lead, hops(cyc[r], lead))
            mine = s[G, far]
            other = mine[G, mate[r]]
            swap = np.where(OWN < mate[r], mine < other, other < mine)
            new = cyc[r][G, np.where(swap, mate[r], OWN)]
            back = np.argsort(new, axis=1)
            z = mx_ref.quantize(((gcols(t[r], new).astype(np.float32) + gcols(t[p], far).astype(np.float32)) * np.float32(0.5)).astype(BF))
            res = [mx_ref.matmul(pick(lay[r], np.arange(128 * b, 128 * b + 128)), z) * np.float32(0.03125) for b in range(4)]
            made.append(tile([(t[r][:, b::4].astype(np.float32) + gpick(res[b], back)) * np.float32(0.5) for b in range(4)]))
            after.append(new)
        now, cyc = made, after
    y, nl = np.zeros((N, 128, C), np.float32), np.zeros((N, 8, C), np.float32)
    oc, osc = np.zeros((N, 128, 4 * C), np.uint8), np.zeros((N, 16, C), np.uint8)
    for r in range(N):
        q = mx_ref.quantize(now[r])
        y[r] = mx_ref.matmul(mx_ref.quantize(v[r]), q)
        nl[r] = cyc[r]
        oc[r], osc[r] = emit(q)
    return {"y": y, "nl": nl, "oc": oc, "osc": osc}

@@ -1,0 +1,461 @@
+from concourse.mybir import dt, AluOpType as A, ActivationFunctionType as AF
+
+C = 320
+ROUNDS = 3
+MASKS = (1, 2, 4)
+MID = 160
+TINY = 2.0 ** -102
+STEPB = 12
+UNIT = 2048.0
+
+NF, NB, NT, NI, NU = 32, 118, 54, 16, 36
+SCRATCH = {
+    "rowf": ("sbuf", [128, C * NF], "float32"),
+    "rowb": ("sbuf", [128, C * NB], "bfloat16"),
+    "tabf": ("sbuf", [128, 20 * NT], "float32"),
+    "tabi": ("sbuf", [128, 20 * NI], "int32"),
+    "tabu": ("sbuf", [128, 20 * NU], "uint16"),
+    "fli": ("sbuf", [128, 20], "int32"),
+    "mli": ("sbuf", [128, 20], "int32"),
+    "jm": ("sbuf", [128, 2 * C], "float32"),
+    "dcon": ("sbuf", [128, 2 * C], "bfloat16"),
+    "pcol": ("sbuf", [128, 8], "int32"),
+    "pcolf": ("sbuf", [128, 16], "float32"),
+    "ui": ("sbuf", [128, 8], "int32"),
+    "u16": ("sbuf", [128, 8], "uint16"),
+    "half": ("sbuf", [128, 512], "bfloat16"),
+    "et": ("sbuf", [128, 2048], "bfloat16"),
+    "eq": ("sbuf", [128, 512], "float8_e4m3fn_x4"),
+    "es": ("sbuf", [128, 512], "uint8"),
+    "uin": ("sbuf", [128, 512], "bfloat16"),
+    "vin": ("sbuf", [128, 512], "bfloat16"),
+    "xin": ("sbuf", [128, 4 * C], "bfloat16"),
+    "uq": ("sbuf", [128, 128], "float8_e4m3fn_x4"),
+    "us": ("sbuf", [128, 128], "uint8"),
+    "up": ("sbuf", [128, 128], "float8_e4m3fn_x4"),
+    "ups": ("sbuf", [128, 128], "uint8"),
+    "vq": ("sbuf", [128, 128], "float8_e4m3fn_x4"),
+    "vs": ("sbuf", [128, 128], "uint8"),
+    "wq": ("sbuf", [128, 512], "float8_e4m3fn_x4"),
+    "wsc": ("sbuf", [128, 512], "uint8"),
+    "ys": ("sbuf", [128, C], "float32"),
+    "nls": ("sbuf", [128, C], "float32"),
+    "ps": ("psum", [128, 512 * 8], "float32"),
+}
+for _r in range(ROUNDS + 1):
+    SCRATCH["xq%d" % _r] = ("sbuf", [128, C], "float8_e4m3fn_x4")
+    SCRATCH["xs%d" % _r] = ("sbuf", [128, C], "uint8")
+for _r in range(ROUNDS):
+    SCRATCH["lq%d" % _r] = ("sbuf", [128, C], "float8_e4m3fn_x4")
+    SCRATCH["ls%d" % _r] = ("sbuf", [128, C], "uint8")
+    SCRATCH["la%d" % _r] = ("sbuf", [128, 60], "uint16")
+    SCRATCH["lb%d" % _r] = ("sbuf", [128, 20], "uint16")
+    SCRATCH["sa%d" % _r] = ("sbuf", [128, 80], "uint16")
+    SCRATCH["sb%d" % _r] = ("sbuf", [128, 20], "uint16")
+for _h in range(2):
+    for _k in ("fh", "fs", "gp", "zt", "xt"): SCRATCH["%s%d" % (_k, _h)] = ("sbuf", [128, 4 * C], "bfloat16")
+    SCRATCH["rs%d" % _h] = ("sbuf", [128, 4 * C], "float32")
+    SCRATCH["zq%d" % _h] = ("sbuf", [128, C], "float8_e4m3fn_x4")
+    SCRATCH["zs%d" % _h] = ("sbuf", [128, C], "uint8")
+
+LOADS = ("fl", "ml", "x", "u", "v", "wc", "ws")
+STORES = ("oc", "os0", "os1", "os2", "os3", "y", "nl")
+SEMAPHORES = ["ev", "es", "et", "eg", "rl"] + ["ld_" + n for n in LOADS] + ["st_" + n for n in STORES] \
+    + ["%s%d" % (k, r) for k in ("aq", "aa", "ab") for r in range(ROUNDS)]
+
+CY, GA, WAKE = 0.83 * 1.2, 1.5, 80.0
+VB, LOOK, PW = 700.0, 150.0, 5.0
+
+
+def add(P, cost, call, reads, writes, sem=None, val=16, after=(), lat=0.0):
+    i = len(P["ops"])
+    deps = set(after)
+    for k in reads:
+        if k in P["last"]: deps.add(P["last"][k])
+    for k in writes:
+        deps.update(P["readers"].get(k, []))
+        if k in P["last"]: deps.add(P["last"][k])
+    for k in reads: P["readers"].setdefault(k, []).append(i)
+    for k in writes:
+        P["last"][k] = i
+        P["readers"][k] = []
+    P["ops"].append({"c": cost, "f": call, "d": sorted(deps), "sem": sem, "val": val, "lat": lat})
+    return i
+
+
+def order(P):
+    ops = P["ops"]
+    n = len(ops)
+    succ = [[] for _ in range(n)]
+    for i in range(n):
+        for j in ops[i]["d"]: succ[j].append(i)
+    way = [0.0] * n
+    for i in range(n - 1, -1, -1):
+        best = 0.0
+        for s in succ[i]: best = max(best, way[s] + WAKE)
+        way[i] = best + min(ops[i]["c"].values()) + ops[i]["lat"]
+    free = {"v": 0.0, "s": 0.0, "t": 0.0, "g": 0.0, "y": 0.0}
+    done, seq = [0.0] * n, []
+    left = [len(o["d"]) for o in ops]
+    at = {}
+
+    def open_(i):
+        at[i] = max([done[j] + WAKE for j in ops[i]["d"]], default=0.0)
+    for i in range(n):
+        if left[i] == 0: open_(i)
+    while at:
+        cand = []
+        for i, t in at.items():
+            c = ops[i]["c"]
+            if len(c) == 1:
+                e = next(iter(c))
+            else:
+                e = "s" if max(t, free["s"]) + c["s"] <= max(t, free["v"]) + c["v"] + VB else "v"
+            cand.append((t if e == "n" else max(t, free[e]), i, e))
+        t0 = min(x[0] for x in cand)
+        eng = max((x for x in cand if x[0] <= t0), key=lambda x: way[x[1]])[2]
+        st, i, e = max((x for x in cand if x[2] == eng and x[0] <= t0 + LOOK), key=lambda x: way[x[1]] - PW * (x[0] - t0))
+        del at[i]
+        c = ops[i]["c"][e]
+        if e != "n": free[e] = st + c
+        done[i] = st + c + ops[i]["lat"]
+        seq.append((st, i, e))
+        for s in succ[i]:
+            left[s] -= 1
+            if left[s] == 0: open_(s)
+    return seq, done
+
+
+def emit(P, g, T, seq):
+    ops = P["ops"]
+    queue = {"v": g.vector, "s": g.scalar, "t": g.tensor, "g": g, "y": g.sync}
+    name = {"v": "ev", "s": "es", "t": "et", "g": "eg"}
+    count = {e: 0 for e in name}
+    know = {e: {} for e in queue}
+    clock, own = {}, {}
+    for st, i, e in seq:
+        o = ops[i]
+        if e == "n":
+            clock[i], own[i] = {o["sem"]: o["val"]}, (o["sem"], o["val"])
+            continue
+        want = {}
+        for j in o["d"]:
+            s, v = own[j]
+            if v and know[e].get(s, 0) < v: want[s] = max(want.get(s, 0), v)
+        for j in o["d"]:
+            s, v = own[j]
+            if want.get(s, 0) >= v > 0:
+                for k, x in clock[j].items():
+                    if k != s and k in want and want[k] <= x: del want[k]
+        for s, v in want.items():
+            queue[e].wait_ge(T.sem[s], v)
+            know[e][s] = v
+        for j in o["d"]:
+            for k, x in clock[j].items(): know[e][k] = max(know[e].get(k, 0), x)
+        ins = o["f"](e)
+        clock[i] = dict(know[e])
+        if o["sem"] is None:
+            count[e] += 1
+            own[i] = (name[e], count[e])
+            ins.then_inc(T.sem[name[e]], 1)
+        else:
+            own[i] = (o["sem"], o["val"])
+            if o["val"]: ins.then_inc(T.sem[o["sem"]], o["val"])
+        if own[i][1]: clock[i][own[i][0]] = own[i][1]
+    return count
+
+
+def rank_program(g, core, T, topo):
+    rank = T.rank_of(core)
+    if rank is None: return
+    P = {"ops": [], "last": {}, "readers": {}}
+    slots = {"rowf": {}, "rowb": {}, "tabf": {}, "tabi": {}, "tabu": {}}
+    top = {k: 0 for k in slots}
+
+    def view(buf, unit, nm, w, a, b, s):
+        d = slots[buf]
+        if nm not in d:
+            d[nm] = top[buf]
+            top[buf] += (w + unit - 1) // unit * unit
+        o = d[nm]
+        b = w if b is None else b
+        return T[buf][:, o + a:o + b:s] if s else T[buf][:, o + a:o + b]
+
+    def F(nm, w=C, a=0, b=None, s=None): return view("rowf", C, nm, w, a, b, s)
+    def B(nm, w=C, a=0, b=None, s=None): return view("rowb", C, nm, w, a, b, s)
+    def tf(nm, w=20, a=0, b=None): return view("tabf", 20, nm, w, a, b, None)
+    def ti(nm, w=20, a=0, b=None): return view("tabi", 20, nm, w, a, b, None)
+    def tu(nm, w=20, a=0, b=None): return view("tabu", 20, nm, w, a, b, None)
+
+    def ts(out, in0, s1, s2, op0, op1, rd, wr, n=20):
+        def call(e): return g.vector.tensor_scalar(out, in0, s1, None, op0) if op1 is None else g.vector.tensor_scalar(out, in0, s1, s2, op0, op1)
+        return add(P, {"v": max(60.0, n * CY)}, call, rd, wr)
+
+    def tt(out, a, b, op, rd, wr, n=20, ind=False):
+        return add(P, {"v": 55 + n * CY * GA if ind else max(60.0, 2 * n * CY)}, lambda e: g.vector.tensor_tensor(out, a, b, op), rd, wr)
+
+    def scan(out, d0, d1, init, op0, op1, rd, wr, n=C, half=False):
+        return add(P, {"v": n * CY * (0.5 if half else 1.0)}, lambda e: g.vector.tensor_tensor_scan(out, d0, d1, init, op0, op1), rd, wr)
+
+    def vcopy(out, in_, rd, wr, n=20): return add(P, {"v": max(60.0, n * CY)}, lambda e: g.vector.tensor_copy(out, in_), rd, wr)
+
+    def scatter(out, in_, rd, wr): return add(P, {"v": 1300.0}, lambda e: g.vector.tensor_copy(out, in_), rd, wr)
+
+    def act(out, in_, func, rd, wr, scale=1.0, bias=None, ind=False):
+        def call(e): return g.scalar.activation(out, in_, func, scale=scale) if bias is None else g.scalar.activation(out, in_, func, bias=bias, scale=scale)
+        return add(P, {"s": 68 + C * CY * GA if ind else C * CY}, call, rd, wr)
+
+    def either(call, rd, wr, ind, n=C): return add(P, {"v": 55 + n * CY * GA, "s": 68 + n * CY * GA} if ind else {"v": n * CY, "s": n * CY}, call, rd, wr)
+
+    def move(out, in_, rd, wr, ind=False, scale=None):
+        def call(e):
+            if e == "s": return g.scalar.activation(out, in_, AF.Copy) if scale is None else g.scalar.activation(out, in_, AF.Copy, scale=scale)
+            return g.vector.tensor_copy(out, in_) if scale is None else g.vector.tensor_scalar(out, in_, scale, None, A.mult)
+        return either(call, rd, wr, ind)
+
+    def affine(out, in_, a, b, rd, wr, ind=False):
+        def call(e):
+            if e == "s": return g.scalar.activation(out, in_, AF.Identity, bias=b, scale=a)
+            return g.vector.tensor_scalar(out, in_, a, b, A.mult, A.add)
+        return either(call, rd, wr, ind)
+
+    def shift(out, in_, x, rd, wr):
+        def call(e):
+            if e == "s": return g.scalar.activation(out, in_, AF.Identity, bias=x)
+            return g.vector.tensor_scalar(out, in_, x, None, A.add)
+        return either(call, rd, wr, False)
+
+    def quant(q, s, in_, n, rd, wr): return add(P, {"v": 12 + 0.22 * 4 * n * 1.2}, lambda e: g.vector.quantize_mx(q, s, in_), rd, wr)
+
+    def bank(b): return T.ps[:, 512 * b:512 * b + C]
+
+    def mm(b, w, ws, x, xs, rd):
+        return add(P, {"t": 1.4 * 0.83 * (C + 16)}, lambda e: g.tensor.matmul_mx(bank(b), w, ws, x, xs, True, True), rd, ["ps%d" % b])
+
+    def load(q, nm, out, in_):
+        return add(P, {q: 60.0}, lambda e: (g.sync if e == "y" else g.scalar).dma_start(out, in_), [], [nm], sem="ld_" + nm, lat=2300.0)
+
+    load("y", "fl", T.fli[:], T.fl[:, :])
+    load("y", "ml", T.mli[:], T.ml[:, :])
+    load("s", "x", T.xin[:], T.x[:, :])
+    load("y", "u", T.uin[:], T.u[:, :])
+    load("y", "wc", T.wq[:].bitcast(dt.uint8), T.wc[:, :])
+    load("y", "ws", T.wsc[:], T.ws[:, :])
+    load("y", "v", T.vin[:], T.v[:, :])
+
+    def iota(out, pat, base, cm, wr, n, fl):
+        def call(e): return g.iota(out, pat, base, cm, allow_small_or_imprecise_dtypes=True) if fl else g.iota(out, pat, base, cm)
+        return add(P, {"g": 130 + 2 * n * CY}, call, [], wr)
+    iota(T.pcol[:, 0:1], [[1, 1]], 0, 1, ["pcol"], 1, False)
+    iota(F("iof"), [[1, C]], 0, 0, ["iof"], C, True)
+    iota(T.jm[:], [[0, 40], [1, 16]], 0, 0, ["jm"], 2 * C, True)
+    iota(T.ui[:], [[16, 8]], 0, 0, ["ui"], 8, False)
+    ts(B("iob"), F("iof"), -float(MID), TINY, A.add, A.mult, ["iof"], ["iob"], C)
+    pc, pf = T.pcol, T.pcolf
+    for b in range(4):
+        ts(pc[:, b + 1:b + 2], pc[:, 0:1], b, 1, A.logical_shift_right, A.bitwise_and, ["pcol"], ["pb%d" % b])
+        ts(pf[:, b:b + 1], pc[:, b + 1:b + 2], 2.0 ** (STEPB << b) - 1, 1.0, A.mult, A.add, ["pb%d" % b], ["pf%d" % b])
+    tt(pf[:, 4:5], pf[:, 0:1], pf[:, 1:2], A.mult, ["pf0", "pf1"], ["pf4"])
+    ts(pf[:, 5:6], pf[:, 2:3], 2.0 ** (102 - 15 * STEPB), None, A.mult, None, ["pf2"], ["pf5"])
+    tt(pf[:, 6:7], pf[:, 3:4], pf[:, 5:6], A.mult, ["pf3", "pf5"], ["pf6"])
+    tt(pf[:, 7:8], pf[:, 4:5], pf[:, 6:7], A.mult, ["pf4", "pf6"], ["sc"])
+    SC = pf[:, 7:8]
+    ts(pc[:, 5:6], pc[:, 0:1], 15, None, A.bitwise_and, None, ["pcol"], ["p15"])
+    vcopy(pf[:, 8:9], pc[:, 5:6], ["p15"], ["p15f"])
+    ts(T.dcon[:], T.jm[:], pf[:, 8:9], 2.0 ** STEPB, A.is_gt, A.mult, ["jm", "p15f"], ["dcon"], 2 * C)
+    ts(F("lab"), F("iof"), UNIT * TINY, -(MID + 1) * TINY, A.mult, A.add, ["iof"], ["lab"], C)
+    for h in range(2):
+        add(P, {"v": 150.0}, lambda e, h=h: g.vector.memset(B("eb%d" % h, 2 * C, 0, C + 16), -MID * TINY), [], ["eb%d" % h])
+    add(P, {"v": 250.0}, lambda e: g.vector.memset(T.half[:], 0.5), [], ["half"])
+    for b in range(4):
+        add(P, {"g": 170 + 1024 * CY}, lambda e, b=b: g.affine_select(T.et[:, 512 * b:512 * b + 512], T.half[:], [[1, 512]], A.is_equal, 0.0, -b, -4),
+            ["half"], ["et%d" % b])
+        quant(T.eq[:, 128 * b:128 * b + 128], T.es[:, 128 * b:128 * b + 128], T.et[:, 512 * b:512 * b + 512], 128, ["et%d" % b], ["eq%d" % b])
+
+    quant(T.xq0[:], T.xs0[:], T.xin[:], C, ["x"], ["X0"])
+    vcopy(T.u16[:], T.ui[:], ["ui"], ["u16"])
+    quant(T.uq[:], T.us[:], T.uin[:], 128, ["u"], ["uq"])
+    add(P, {"v": 250.0}, lambda e: g.vector.tensor_copy(T.up[:].bitcast(dt.uint32), T.uq[:].bitcast(dt.uint32).indirect(T.u16[:])), ["uq", "u16"], ["up"])
+    add(P, {"v": 250.0}, lambda e: g.vector.tensor_copy(T.ups[:], T.us[:].indirect(T.u16[:])), ["uq", "u16"], ["ups"])
+    quant(T.vq[:], T.vs[:], T.vin[:], 128, ["v"], ["vq"])
+
+    def compact(out, nm, bias, rd, wr, w=1):
+        n = w * C
+        scan(B(nm + "k", n), T.dcon[:, 0:n], B(nm, n), 0.0, A.mult, A.add, rd + ["dcon"], [nm + "k"], n, True)
+        if out is not None: ts(out, B(nm + "k", n, 15, n, 16), SC, bias, A.mult, A.add, [nm + "k", "sc"], wr, 20 * w)
+
+    vcopy(tu("LG0", 40, 0, 20), T.fli[:], ["fl"], ["L0_0"])
+    vcopy(tu("M16"), T.mli[:], ["ml"], ["M16"])
+    scatter(B("gl0").indirect(tu("LG0", 40, 0, 20)), B("iob"), ["L0_0", "iob"], ["gl0"])
+    compact(tu("LG0", 40, 20, 40), "gl0", MID + 0.25, ["gl0"], ["GL_0"])
+    move(B("mr"), B("iob").indirect(tu("M16")), ["iob", "M16"], ["mr"], ind=True)
+    tt(F("sgd"), B("mr"), B("iob"), A.subtract, ["mr", "iob"], ["sgd"], C)
+    act(F("sg"), F("sgd"), AF.Sign, ["sgd"], ["sg"], scale=2.0 ** 97)
+
+    sent = [0]
+    for r in range(ROUNDS):
+        h = r % 2
+        R = lambda nm: "%s_%d" % (nm, h)
+        partner = T.cores[rank ^ MASKS[r]]
+        rid, pid, _s = topo.addr(partner)
+        msk, ne, na = topo.mask(core, partner), len(topo.engines(core, partner)), len(topo.engines(partner, core))
+        X, Xq, Xs = "X%d" % r, T["xq%d" % r], T["xs%d" % r]
+
+        def send(sem, pieces, rd, key, lat):
+            for dst, src in pieces:
+                last = add(P, {"g": 300.0}, lambda e, dst=dst, src=src, sem=sem, rid=rid, pid=pid, msk=msk: g.remote_dma(dst, src, T.sem[sem], T.sem.rl, pid, rid, msk),
+                           rd, ["net"], sem="rl", val=0)
+                sent[0] += ne
+            add(P, {"n": 0.0}, None, [], [key], sem=sem, val=na * len(pieces), after=[last], lat=lat)
+
+        send("aq%d" % r, [(T["lq%d" % r][:].bitcast(dt.uint8), Xq[:].bitcast(dt.uint8)), (T["ls%d" % r][:], Xs[:])], [X], "Y%d" % r, 6000.0)
+
+        mm(0, T.up[:], T.ups[:], Xq[:], Xs[:], ["up", "ups", X])
+        move(F(R("s")), bank(0), ["ps0"], [R("s")])
+        for b in range(4):
+            mm(1 + b, T.eq[:, 128 * b:128 * b + 128], T.es[:, 128 * b:128 * b + 128], Xq[:], Xs[:], ["eq%d" % b, X])
+            move(T["fh%d" % h][:, C * b:C * b + C], bank(1 + b), ["ps%d" % (1 + b)], ["fh%d%d" % (h, b)])
+
+        LG, LN = "LG%d" % r, "LG%d" % (r + 1)
+        FL, GL, FN, GN = "L0_%d" % r, "GL_%d" % r, "L0_%d" % (r + 1), "GL_%d" % (r + 1)
+        fl_, gl_, fn_, gn_ = tu(LG, 40, 0, 20), tu(LG, 40, 20, 40), tu(LN, 40, 0, 20), tu(LN, 40, 20, 40)
+        L = [FL] + [R("L%d" % k) for k in range(1, 8)]
+        lists = [fl_] + [tu(k) for k in L[1:]]
+        move(B(R("fr0")), B("iob").indirect(fl_), ["iob", FL], [R("fr0")], ind=True)
+        for nm, x in (("key0", 0.0), ("w0", 1.0)):
+            affine(F(R(nm)), B("iob").indirect(fl_), UNIT, (UNIT * MID - MID + x) * TINY, ["iob", FL], [R(nm)], ind=True)
+        for k in range(9):
+            if k < 7:
+                nx = R("fr%d" % (k + 1))
+                move(B(nx), B(R("fr%d" % k)).indirect(lists[k]), [R("fr%d" % k), L[k]], [nx], ind=True)
+                compact(lists[k + 1], nx, MID + 0.25, [nx], [L[k + 1]])
+            q = k if k < 8 else 6
+            a, b = R("key%d" % (k % 2)), R("key%d" % ((k + 1) % 2))
+            w, wn = R("w%d" % (k % 2)), R("w%d" % ((k + 1) % 2))
+            tt(F(b), F(w).indirect(lists[q]), F(a), A.min, [w, L[q], a], [b], C, True)
+            if k < 8: shift(F(wn), F(b), (2.0 ** (k + 1) if k < 7 else 64.0) * TINY, [b], [wn])
+        key = R("key1")
+
+        act(B(R("kb")), F(key), AF.Identity, [key], [R("kb")], scale=1 / UNIT, bias=-MID * TINY)
+        RL = R("RL")
+        compact(tu(RL, 40, 0, 20), R("kb"), MID + 0.25, [R("kb")], [RL + "a"])
+        ts(tu(RL, 40, 20, 40), B(R("kb") + "k", C, 15, C, 16), SC, MID + 1.25, A.mult, A.add, [R("kb") + "k", "sc"], [RL + "b"])
+        tt(F(R("mx")), F(key), F("lab"), A.max, [key, "lab"], [R("mx")], C)
+        eb, be = "eb%d" % h, R("be")
+        scan(B(eb, 2 * C, 1, C + 1), F(R("mx")), F("lab"), -MID * TINY, A.add, A.subtract, [R("mx"), "lab"], [eb])
+        big = 1.5 * 2.0 ** 23 * UNIT * TINY
+        act(F(R("ru")), F(key), AF.Identity, [key], [R("ru")], bias=big)
+        act(F(R("rv")), F(R("ru")), AF.Identity, [R("ru")], [R("rv")], bias=-big)
+        tt(B(R("cr")), F(key), F(R("rv")), A.subtract, [key, R("rv")], [R("cr")], C)
+        it = R("it")
+        compact(ti(it, 80, 20, 40), R("cr"), float(MID), [R("cr")], [it + "c"])
+        move(B(be, 2 * C, 0, C), B(eb, 2 * C, 0, C + 1).indirect(tu(RL, 40, 0, 20)), [eb, RL + "a"], [be + "b"], ind=True)
+        affine(B(be, 2 * C, C, 2 * C), B(eb, 2 * C, 0, C + 1).indirect(tu(RL, 40, 20, 40)), 1.0, -TINY, [eb, RL + "b"], [be + "e"], ind=True)
+        compact(ti(it, 80, 40, 80), be, float(MID), [be + "b", be + "e"], [it + "b"], 2)
+        tt(tf(R("pos")), ti(it, 80, 20, 40), ti(it, 80, 40, 60), A.add, [it + "c", it + "b"], [R("pos")])
+        vcopy(tu(R("P16")), tf(R("pos")), [R("pos")], [R("P16")])
+        tt(ti(it, 80, 0, 20), ti(it, 80, 60, 80), ti(it, 80, 40, 60), A.subtract, [it + "b"], [it + "n"])
+        sa, sb, SA, O16 = T["sa%d" % r], T["sb%d" % r], "sa%d" % r, "sb%d" % r
+        vcopy(sa[:], ti(it, 80), [it + "n", it + "c", it + "b"], [SA], 80)
+        E16 = sa[:, 60:80]
+        send("aa%d" % r, [(T["la%d" % r][:], sa[:, 0:60])], [SA], "la%d" % r, 3000.0)
+        ts(tf(R("nf")), ti(it, 80, 0, 20), 1.0, None, A.add, None, [it + "n"], [R("nf")])
+        ol = R("ol")
+        scatter(B(ol).indirect(tu(R("P16"))), B("iob"), [R("P16"), "iob"], [ol])
+        compact(sb[:], ol, MID + 0.25, [ol], [O16])
+        send("ab%d" % r, [(T["lb%d" % r][:], sb[:])], [O16], "lb%d" % r, 3000.0)
+        act(B(R("flag")), B(R("cr")), AF.Relu, [R("cr")], [R("flag")], scale=-2.0 ** 97, bias=(1.0 - MID) * TINY * 2.0 ** 97)
+        act(B(R("d0")), B(R("flag")).indirect(sb[:]), AF.Copy, [R("flag"), O16], [R("d0")], scale=-2.0 ** 97, ind=True)
+        move(B(R("d1")), B(R("d0")), [R("d0")], [R("d1")], scale=-1.0)
+        move(B(R("prow")), B("iob").indirect(tu(R("P16"))), ["iob", R("P16")], [R("prow")], ind=True)
+        fg = R("fg")
+        move(B(fg, 2 * C, 0, C), B(R("fr0")).indirect(tu("M16")), [R("fr0"), "M16"], [fg + "f"], ind=True)
+        move(B(fg, 2 * C, C, 2 * C), B("mr").indirect(gl_), ["mr", GL], [fg + "g"], ind=True)
+        compact(tf(R("fgv"), 40), fg, MID + 0.25, [fg + "f", fg + "g"], [R("fgv")], 2)
+        ts(tf(R("fg0"), 40), tu(LG, 40), 0.25, None, A.add, None, [FL, GL], [R("fg0")], 40)
+        tt(tf(R("fgd"), 40), tf(R("fgv"), 40), tf(R("fg0"), 40), A.subtract, [R("fgv"), R("fg0")], [R("fgd")], 40)
+        ts(tf(R("fgs"), 40), tf(R("fgd"), 40), SC, None, A.mult, None, [R("fgd"), "sc"], [R("fgs")], 40)
+
+        move(F(R("so")), F(R("s")).indirect(sb[:]), [R("s"), O16], [R("so")], ind=True)
+        scan(F(R("pm")), B(R("d0")), F(R("so")), -2.0 ** 92, A.add, A.max, [R("d0"), R("so")], [R("pm")])
+        tt(F(R("eq")), F(R("pm")).indirect(E16), F(R("s")), A.subtract, [R("pm"), SA, R("s")], [R("eq")], C, True)
+        tt(B(R("cd")), F(R("eq")).indirect(sb[:]), B(ol), A.add, [R("eq"), O16, ol], [R("cd")], C, True)
+        scan(B(R("cs")), B(R("d1")), B(R("cd")), 0.0, A.add, A.min, [R("d1"), R("cd")], [R("cs")], C, True)
+        move(B(R("gk")), B(R("cs")).indirect(E16), [R("cs"), SA], [R("gk")], ind=True)
+        l16 = R("l16")
+        compact(tu(l16), R("gk"), MID + 0.25, [R("gk")], [l16])
+
+        xa = R("xa")
+        for q in range(3):
+            move(B(xa, 3 * C, C * q, C * q + C), B("iob").indirect(T["la%d" % r][:, 20 * q:20 * q + 20]), ["iob", "la%d" % r], [xa + str(q)], ind=True)
+        move(B(R("oe")), B("iob").indirect(T["lb%d" % r][:]), ["iob", "lb%d" % r], [R("oe")], ind=True)
+        move(B(R("xn")), B(xa, 3 * C, 0, C).indirect(tu(l16)), [xa + "0", l16], [R("xn")], ind=True)
+        compact(ti(R("xni")), R("xn"), MID + 1.0, [R("xn")], [R("xni")])
+        xd = R("xd")
+        for q in (1, 2): move(B(xd, 2 * C, C * q - C, C * q), B(xa, 3 * C, C * q, C * q + C).indirect(tu(l16)), [xa + str(q), l16], [xd + str(q)], ind=True)
+        compact(ti(R("xdi"), 40), xd, float(MID), [xd + "1", xd + "2"], [R("xdi")], 2)
+        move(B(R("xp")), B(R("prow")).indirect(tu(l16)), [R("prow"), l16], [R("xp")], ind=True)
+        compact(tf(R("pl")), R("xp"), MID - 0.5, [R("xp")], [R("pl")])
+        tt(tf(R("dl")), tf(R("pl")), tf(R("pos")), A.subtract, [R("pl"), R("pos")], [R("dl")])
+        ts(tf(R("ng")), tf(R("dl")), -0.75, None, A.is_lt, None, [R("dl")], [R("ng")])
+        tt(tf(R("nn")), tf(R("ng")), tf(R("nf")), A.mult, [R("ng"), R("nf")], [R("nn")])
+        vcopy(tf(R("ne")), ti(R("xni")), [R("xni")], [R("ne")])
+        add(P, {"v": 300.0}, lambda e, a=R("rn"), b=R("ne"): g.vector.reciprocal(tf(a), tf(b)), [R("ne")], [R("rn")])
+        tt(tf(R("z0")), ti(R("xdi"), 40, 0, 20), tf(R("dl")), A.subtract, [R("xdi"), R("dl")], [R("z0")])
+        tt(tf(R("zh")), tf(R("z0")), tf(R("nn")), A.subtract, [R("z0"), R("nn")], [R("zh")])
+        tt(tf(R("tq")), tf(R("zh")), tf(R("rn")), A.mult, [R("zh"), R("rn")], [R("tq")])
+        ts(ti(R("qi")), tf(R("tq")), -0.5, None, A.add, None, [R("tq")], [R("qi")])
+        tt(tf(R("zb")), tf(R("zh")), ti(R("xdi"), 40, 20, 40), A.add, [R("zh"), R("xdi")], [R("zb")])
+        tt(tf(R("m1")), ti(R("qi")), tf(R("ne")), A.mult, [R("qi"), R("ne")], [R("m1")])
+        tt(tf(R("pp")), tf(R("zb")), tf(R("m1")), A.subtract, [R("zb"), R("m1")], [R("pp")])
+        ts(tu(R("PL")), tf(R("pp")), -0.25, None, A.add, None, [R("pp")], [R("PL")])
+        move(B(R("tr")), B(R("oe")).indirect(tu(R("PL"))), [R("oe"), R("PL")], [R("tr")], ind=True)
+        T16 = R("T16")
+        compact(tu(T16), R("tr"), MID + 0.25, [R("tr")], [T16])
+
+        tt(F(R("st")), F(R("s")).indirect(tu(T16)), F("sg"), A.mult, [R("s"), T16, "sg"], [R("st")], C, True)
+        for c in range(2):
+            a, b = C // 2 * c, C // 2 * c + C // 2
+            either(lambda e, o=F(R("su"), C, a, b), i=F(R("st"), C, a, b): g.vector.tensor_copy(o, i) if e == "v" else g.scalar.activation(o, i, AF.Copy),
+                   [R("st")], [R("su") + "ab"[c]], False, C // 2)
+        tt(F(R("sv")), F(R("st")).indirect(tu("M16")), F(R("su")), A.add, [R("st"), R("su") + "a", R("su") + "b", "M16"], [R("sv")], C, True)
+        ts(B(R("sw")), F(R("sv")), 0.0, TINY, A.is_lt, A.mult, [R("sv")], [R("sw")], C)
+        move(B(R("swg")), B(R("sw")).indirect(gl_), [R("sw"), GL], [R("swg")], ind=True)
+        for nm, a, out, kk in (("sw", 0, fn_, FN), ("swg", 20, gn_, GN)):
+            compact(None, R(nm), 0.0, [R(nm)], None)
+            tt(tf(R(nm + "x")), B(R(nm) + "k", C, 15, C, 16), tf(R("fgs"), 40, a, a + 20), A.mult, [R(nm) + "k", R("fgs")], [R(nm + "x")])
+            tt(tf(R(nm + "y")), tf(R(nm + "x")), tf(R("fg0"), 40, a, a + 20), A.add, [R(nm + "x"), R("fg0")], [R(nm + "y")])
+            vcopy(out, tf(R(nm + "y")), [R(nm + "y")], [kk])
+
+        fh, fs, gp, zt, xt, rs = [T["%s%d" % (k, h)] for k in ("fh", "fs", "gp", "zt", "xt", "rs")]
+        for b in range(4):
+            bk, c = (5, 6, 7, 0)[b], slice(C * b, C * b + C)
+            mm(bk, T.eq[:, 128 * b:128 * b + 128], T.es[:, 128 * b:128 * b + 128], T["lq%d" % r][:], T["ls%d" % r][:], ["eq%d" % b, "Y%d" % r])
+            move(fs[:, c], bank(bk), ["ps%d" % bk], ["fs%d%d" % (h, b)])
+            move(gp[:, c], fs[:, c].indirect(tu(T16)), ["fs%d%d" % (h, b), T16], ["gp%d%d" % (h, b)], ind=True)
+            tt(zt[:, b:4 * C:4], fh[:, c].indirect(fn_), gp[:, c], A.add, ["fh%d%d" % (h, b), FN, "gp%d%d" % (h, b)], ["zt%d%d" % (h, b)], C, True)
+        zq, zs = T["zq%d" % h], T["zs%d" % h]
+        quant(zq[:], zs[:], zt[:], C, ["zt%d%d" % (h, b) for b in range(4)], ["zq%d" % h])
+        for b in range(4):
+            c = slice(C * b, C * b + C)
+            mm(1 + b, T.wq[:, 128 * b:128 * b + 128], T.wsc[:, 128 * b:128 * b + 128], zq[:], zs[:], ["wc", "ws", "zq%d" % h])
+            move(rs[:, c], bank(1 + b), ["ps%d" % (1 + b)], ["rs%d%d" % (h, b)], scale=2.0 ** -6)
+            tt(xt[:, b:4 * C:4], rs[:, c].indirect(gn_), fh[:, c], A.add, ["rs%d%d" % (h, b), GN, "fh%d%d" % (h, b)], ["xt%d%d" % (h, b)], C, True)
+        quant(T["xq%d" % (r + 1)][:], T["xs%d" % (r + 1)][:], xt[:], C, ["xt%d%d" % (h, b) for b in range(4)], ["X%d" % (r + 1)])
+
+    q, s, X = T["xq%d" % ROUNDS], T["xs%d" % ROUNDS], "X%d" % ROUNDS
+
+    def store(nm, out, in_, rd): add(P, {"y": 60.0}, lambda e: g.sync.dma_start(out, in_), rd, [], sem="st_" + nm, lat=2000.0)
+    act(T.nls[:], F("iof").indirect(tu("LG%d" % ROUNDS, 40, 0, 20)), AF.Copy, ["iof", "L0_%d" % ROUNDS], ["nls"], ind=True)
+    store("nl", T.nl[:, :], T.nls[0:128:16, :], ["nls"])
+    mm(1, T.vq[:], T.vs[:], q[:], s[:], ["vq", X])
+    move(T.ys[:], bank(1), ["ps1"], ["ys"])
+    store("oc", T.oc[:, :], q[:].bitcast(dt.uint8), [X])
+    for k in range(4): store("os%d" % k, T.osc[4 * k:4 * k + 4, :], s[32 * k:32 * k + 4, :], [X])
+    store("y", T.y[:, :], T.ys[:], ["ys"])
+
+    seq, done = order(P)
+    count = emit(P, g, T, seq)
+    for nm in STORES: g.sync.wait_ge(T.sem["st_" + nm], 16)
+    g.wait_ge(T.sem.rl, sent[0])
+    for e, nm in (("v", "ev"), ("s", "es"), ("t", "et"), ("g", "eg")): g.sync.wait_ge(T.sem[nm], count[e])

@@ -8,7 +8,7 @@ TINY = 2.0 ** -102
 STEPB = 12
 UNIT = 2048.0
 
-NF, NB, NT, NI, NU = 32, 118, 54, 16, 36
+NF, NB, NT, NI, NU = 34, 118, 54, 18, 36
 SCRATCH = {
     "rowf": ("sbuf", [128, C * NF], "float32"),
     "rowb": ("sbuf", [128, C * NB], "bfloat16"),
@@ -63,8 +63,10 @@ STORES = ("oc", "os0", "os1", "os2", "os3", "y", "nl")
 SEMAPHORES = ["ev", "es", "et", "eg", "rl"] + ["ld_" + n for n in LOADS] + ["st_" + n for n in STORES] \
     + ["%s%d" % (k, r) for k in ("aq", "aa", "ab") for r in range(ROUNDS)]
 
-CY, GA, WAKE = 0.83 * 1.2, 1.5, 80.0
-VB, LOOK, PW = 700.0, 150.0, 5.0
+CY, GA, WAKE = 0.83 * 1.2, 1.5, 130.0
+VB, LOOK, PW = 500.0, 150.0, 5.0
+OFFS = "imdgjjbagglflfmjmjmjfhfbjgaggadgcabadamlfgfliaaefgcgfafhhmmgbhdgalbjdeadbmabldmfkmchgagjcmfmlajmamkmafmigcmdlihghblhcckekacmgeehjbiaahifjabajfgdagjmigacmiaakjmgfhjhjlihgcaagaaajbklmmifjadkelmgdgaagflhcimfajflmfmjedhdfgaimfmmhelghmjkhkmgemfkfgejeblmlkmfjhljlmmdmaaimfeigeccjmdlblcgjkbkhikhfgfafjbggfekaddhaamfgfegllajgaamgbmlfihiiaihgjklgmjhhhghgigaaaigajlckmakmammbadbgjkmkcliejmkcmeccbjaedjkkhffmjggcmjhadmikglamgkaahmfgmfbgaimaagjfkmmddafjgaecajbflhjelammlcmdeafjmlkjmhejdhbjikaddfajkgiiafdaadfbgfggflegkjeelmfgefeeffmccdbhbegkdbagmgekechddajdfmmahfmaddllhggblmmgegmamlecmhmehgljm"
+FLEX = "----------------------------------------------------------------s-v---sv-----s---ss---------s---ss----s---s-s------------ss---------------sss--------------s--s--v------------------------s--s----------s---s--------------s--------------s---s-s---s---ss---ss----s---s----------------s-------------s---------------s------------v-----sv--s---v-------------------vs------------s---ss--ss--s-------v--s--s------s---s---sssss---ss---s-----s---s----ss---ss-----s------------------------------s------v-------s-vsv---v--s-------------------v-------------s---s----s--ss------s--s--s------------"
 
 
 def add(P, cost, call, reads, writes, sem=None, val=16, after=(), lat=0.0):
@@ -94,6 +96,7 @@ def order(P):
         best = 0.0
         for s in succ[i]: best = max(best, way[s] + WAKE)
         way[i] = best + min(ops[i]["c"].values()) + ops[i]["lat"]
+    way = [x + 500.0 * (ord(OFFS[i]) - 103) if i < len(OFFS) else x for i, x in enumerate(way)]
     free = {"v": 0.0, "s": 0.0, "t": 0.0, "g": 0.0, "y": 0.0}
     done, seq = [0.0] * n, []
     left = [len(o["d"]) for o in ops]
@@ -109,8 +112,12 @@ def order(P):
             c = ops[i]["c"]
             if len(c) == 1:
                 e = next(iter(c))
+            elif i < len(FLEX) and FLEX[i] != "-":
+                e = FLEX[i]
             else:
-                e = "s" if max(t, free["s"]) + c["s"] <= max(t, free["v"]) + c["v"] + VB else "v"
+                tv = max(t, free["v"])
+                busy = any(len(ops[j]["c"]) == 1 and "v" in ops[j]["c"] and u <= tv + c["v"] for j, u in at.items())
+                e = "s" if max(t, free["s"]) + c["s"] <= tv + c["v"] + (VB if busy else 0.0) else "v"
             cand.append((t if e == "n" else max(t, free[e]), i, e))
         t0 = min(x[0] for x in cand)
         eng = max((x for x in cand if x[0] <= t0), key=lambda x: way[x[1]])[2]
@@ -264,7 +271,9 @@ def rank_program(g, core, T, topo):
     vcopy(pf[:, 8:9], pc[:, 5:6], ["p15"], ["p15f"])
     ts(T.dcon[:], T.jm[:], pf[:, 8:9], 2.0 ** STEPB, A.is_gt, A.mult, ["jm", "p15f"], ["dcon"], 2 * C)
     ts(F("lab"), F("iof"), UNIT * TINY, -(MID + 1) * TINY, A.mult, A.add, ["iof"], ["lab"], C)
+    ts(F("lab2"), F("iof"), UNIT * TINY, (UNIT - MID - 1) * TINY, A.mult, A.add, ["iof"], ["lab2"], C)
     for h in range(2):
+        add(P, {"v": 300.0}, lambda e, h=h: g.vector.memset(F("gw%d" % h, 2 * C, 0, C + 8), 0.0), [], ["gw%d" % h])
         add(P, {"v": 150.0}, lambda e, h=h: g.vector.memset(B("eb%d" % h, 2 * C, 0, C + 16), -MID * TINY), [], ["eb%d" % h])
     add(P, {"v": 250.0}, lambda e: g.vector.memset(T.half[:], 0.5), [], ["half"])
     for b in range(4):
@@ -293,12 +302,14 @@ def rank_program(g, core, T, topo):
     act(F("sg"), F("sgd"), AF.Sign, ["sgd"], ["sg"], scale=2.0 ** 97)
 
     sent = [0]
+    peers = [T.cores[rank ^ m] for m in MASKS]
+    common = [e for e in topo.engines(core, peers[0]) if all(e in topo.engines(core, p) and e in topo.engines(p, core) for p in peers)]
     for r in range(ROUNDS):
         h = r % 2
         R = lambda nm: "%s_%d" % (nm, h)
         partner = T.cores[rank ^ MASKS[r]]
         rid, pid, _s = topo.addr(partner)
-        msk, ne, na = topo.mask(core, partner), len(topo.engines(core, partner)), len(topo.engines(partner, core))
+        msk, ne = sum(1 << e for e in common), len(common)
         X, Xq, Xs = "X%d" % r, T["xq%d" % r], T["xs%d" % r]
 
         def send(sem, pieces, rd, key, lat):
@@ -306,9 +317,9 @@ def rank_program(g, core, T, topo):
                 last = add(P, {"g": 300.0}, lambda e, dst=dst, src=src, sem=sem, rid=rid, pid=pid, msk=msk: g.remote_dma(dst, src, T.sem[sem], T.sem.rl, pid, rid, msk),
                            rd, ["net"], sem="rl", val=0)
                 sent[0] += ne
-            add(P, {"n": 0.0}, None, [], [key], sem=sem, val=na * len(pieces), after=[last], lat=lat)
+            add(P, {"n": 0.0}, None, [], [key], sem=sem, val=ne * len(pieces), after=[last], lat=lat)
 
-        send("aq%d" % r, [(T["lq%d" % r][:].bitcast(dt.uint8), Xq[:].bitcast(dt.uint8)), (T["ls%d" % r][:], Xs[:])], [X], "Y%d" % r, 6000.0)
+        send("aq%d" % r, [(T["lq%d" % r][:].bitcast(dt.uint8), Xq[:].bitcast(dt.uint8)), (T["ls%d" % r][:], Xs[:])], [X], "Y%d" % r, 9000.0)
 
         mm(0, T.up[:], T.ups[:], Xq[:], Xs[:], ["up", "ups", X])
         move(F(R("s")), bank(0), ["ps0"], [R("s")])
@@ -343,31 +354,29 @@ def rank_program(g, core, T, topo):
         tt(F(R("mx")), F(key), F("lab"), A.max, [key, "lab"], [R("mx")], C)
         eb, be = "eb%d" % h, R("be")
         scan(B(eb, 2 * C, 1, C + 1), F(R("mx")), F("lab"), -MID * TINY, A.add, A.subtract, [R("mx"), "lab"], [eb])
-        big = 1.5 * 2.0 ** 23 * UNIT * TINY
-        act(F(R("ru")), F(key), AF.Identity, [key], [R("ru")], bias=big)
-        act(F(R("rv")), F(R("ru")), AF.Identity, [R("ru")], [R("rv")], bias=-big)
-        tt(B(R("cr")), F(key), F(R("rv")), A.subtract, [key, R("rv")], [R("cr")], C)
+        gw, prow = "gw%d" % h, R("prow")
+        scan(F(gw, 2 * C, 1, C + 1), F(R("mx")), F("lab2"), 0.0, A.add, A.subtract, [R("mx"), "lab2"], [gw])
+        tt(B(prow), F(gw, 2 * C, 0, C + 1).indirect(tu(RL, 40, 0, 20)), F(key), A.add, [gw, RL + "a", key], [prow], C, True)
+        compact(tu(R("P16")), prow, MID + 0.25, [prow], [R("P16")])
+        ts(ti(R("pos")), B(prow + "k", C, 15, C, 16), SC, float(MID), A.mult, A.add, [prow + "k", "sc"], [R("pos")])
         it = R("it")
-        compact(ti(it, 80, 20, 40), R("cr"), float(MID), [R("cr")], [it + "c"])
         move(B(be, 2 * C, 0, C), B(eb, 2 * C, 0, C + 1).indirect(tu(RL, 40, 0, 20)), [eb, RL + "a"], [be + "b"], ind=True)
         affine(B(be, 2 * C, C, 2 * C), B(eb, 2 * C, 0, C + 1).indirect(tu(RL, 40, 20, 40)), 1.0, -TINY, [eb, RL + "b"], [be + "e"], ind=True)
         compact(ti(it, 80, 40, 80), be, float(MID), [be + "b", be + "e"], [it + "b"], 2)
-        tt(tf(R("pos")), ti(it, 80, 20, 40), ti(it, 80, 40, 60), A.add, [it + "c", it + "b"], [R("pos")])
-        vcopy(tu(R("P16")), tf(R("pos")), [R("pos")], [R("P16")])
+        tt(ti(it, 80, 20, 40), ti(R("pos")), ti(it, 80, 40, 60), A.subtract, [R("pos"), it + "b"], [it + "c"])
         tt(ti(it, 80, 0, 20), ti(it, 80, 60, 80), ti(it, 80, 40, 60), A.subtract, [it + "b"], [it + "n"])
         sa, sb, SA, O16 = T["sa%d" % r], T["sb%d" % r], "sa%d" % r, "sb%d" % r
         vcopy(sa[:], ti(it, 80), [it + "n", it + "c", it + "b"], [SA], 80)
         E16 = sa[:, 60:80]
-        send("aa%d" % r, [(T["la%d" % r][:], sa[:, 0:60])], [SA], "la%d" % r, 3000.0)
+        send("aa%d" % r, [(T["la%d" % r][:], sa[:, 0:60])], [SA], "la%d" % r, 4500.0)
         ts(tf(R("nf")), ti(it, 80, 0, 20), 1.0, None, A.add, None, [it + "n"], [R("nf")])
         ol = R("ol")
         scatter(B(ol).indirect(tu(R("P16"))), B("iob"), [R("P16"), "iob"], [ol])
         compact(sb[:], ol, MID + 0.25, [ol], [O16])
-        send("ab%d" % r, [(T["lb%d" % r][:], sb[:])], [O16], "lb%d" % r, 3000.0)
-        act(B(R("flag")), B(R("cr")), AF.Relu, [R("cr")], [R("flag")], scale=-2.0 ** 97, bias=(1.0 - MID) * TINY * 2.0 ** 97)
+        send("ab%d" % r, [(T["lb%d" % r][:], sb[:])], [O16], "lb%d" % r, 4500.0)
+        act(B(R("flag")), B("iob").indirect(sa[:, 20:40]), AF.Relu, ["iob", SA], [R("flag")], scale=-2.0 ** 97, bias=(1.0 - MID) * TINY * 2.0 ** 97, ind=True)
         act(B(R("d0")), B(R("flag")).indirect(sb[:]), AF.Copy, [R("flag"), O16], [R("d0")], scale=-2.0 ** 97, ind=True)
         move(B(R("d1")), B(R("d0")), [R("d0")], [R("d1")], scale=-1.0)
-        move(B(R("prow")), B("iob").indirect(tu(R("P16"))), ["iob", R("P16")], [R("prow")], ind=True)
         fg = R("fg")
         move(B(fg, 2 * C, 0, C), B(R("fr0")).indirect(tu("M16")), [R("fr0"), "M16"], [fg + "f"], ind=True)
         move(B(fg, 2 * C, C, 2 * C), B("mr").indirect(gl_), ["mr", GL], [fg + "g"], ind=True)
@@ -393,19 +402,21 @@ def rank_program(g, core, T, topo):
         compact(ti(R("xni")), R("xn"), MID + 1.0, [R("xn")], [R("xni")])
         xd = R("xd")
         for q in (1, 2): move(B(xd, 2 * C, C * q - C, C * q), B(xa, 3 * C, C * q, C * q + C).indirect(tu(l16)), [xa + str(q), l16], [xd + str(q)], ind=True)
-        compact(ti(R("xdi"), 40), xd, float(MID), [xd + "1", xd + "2"], [R("xdi")], 2)
+        compact(None, xd, 0.0, [xd + "1", xd + "2"], None, 2)
+        ts(tf(R("xb")), B(xd + "k", 2 * C, C + 15, 2 * C, 16), SC, float(MID), A.mult, A.add, [xd + "k", "sc"], [R("xb")])
         move(B(R("xp")), B(R("prow")).indirect(tu(l16)), [R("prow"), l16], [R("xp")], ind=True)
-        compact(tf(R("pl")), R("xp"), MID - 0.5, [R("xp")], [R("pl")])
-        tt(tf(R("dl")), tf(R("pl")), tf(R("pos")), A.subtract, [R("pl"), R("pos")], [R("dl")])
-        ts(tf(R("ng")), tf(R("dl")), -0.75, None, A.is_lt, None, [R("dl")], [R("ng")])
+        compact(None, R("xp"), 0.0, [R("xp")], None)
+        tt(tf(R("dl")), B(R("xp") + "k", C, 15, C, 16), B(prow + "k", C, 15, C, 16), A.subtract, [R("xp") + "k", prow + "k"], [R("dl")])
+        ts(tf(R("ng")), tf(R("dl")), SC, -0.5, A.mult, A.is_lt, [R("dl"), "sc"], [R("ng")])
         tt(tf(R("nn")), tf(R("ng")), tf(R("nf")), A.mult, [R("ng"), R("nf")], [R("nn")])
         vcopy(tf(R("ne")), ti(R("xni")), [R("xni")], [R("ne")])
         add(P, {"v": 300.0}, lambda e, a=R("rn"), b=R("ne"): g.vector.reciprocal(tf(a), tf(b)), [R("ne")], [R("rn")])
-        tt(tf(R("z0")), ti(R("xdi"), 40, 0, 20), tf(R("dl")), A.subtract, [R("xdi"), R("dl")], [R("z0")])
+        tt(tf(R("zr")), B(xd + "k", 2 * C, 15, C, 16), tf(R("dl")), A.subtract, [xd + "k", R("dl")], [R("zr")])
+        ts(tf(R("z0")), tf(R("zr")), SC, MID + 0.5, A.mult, A.add, [R("zr"), "sc"], [R("z0")])
         tt(tf(R("zh")), tf(R("z0")), tf(R("nn")), A.subtract, [R("z0"), R("nn")], [R("zh")])
         tt(tf(R("tq")), tf(R("zh")), tf(R("rn")), A.mult, [R("zh"), R("rn")], [R("tq")])
         ts(ti(R("qi")), tf(R("tq")), -0.5, None, A.add, None, [R("tq")], [R("qi")])
-        tt(tf(R("zb")), tf(R("zh")), ti(R("xdi"), 40, 20, 40), A.add, [R("zh"), R("xdi")], [R("zb")])
+        tt(tf(R("zb")), tf(R("zh")), tf(R("xb")), A.add, [R("zh"), R("xb")], [R("zb")])
         tt(tf(R("m1")), ti(R("qi")), tf(R("ne")), A.mult, [R("qi"), R("ne")], [R("m1")])
         tt(tf(R("pp")), tf(R("zb")), tf(R("m1")), A.subtract, [R("zb"), R("m1")], [R("pp")])
         ts(tu(R("PL")), tf(R("pp")), -0.25, None, A.add, None, [R("pp")], [R("PL")])

from concourse.mybir import dt, AluOpType as A, ActivationFunctionType as AF

C = 320
ROUNDS = 3
MASKS = (1, 2, 4)
MID = 160
TINY = 2.0 ** -102
STEPB = 12
UNIT = 2048.0

NF, NB, NT, NI, NU = 34, 118, 54, 18, 36
SCRATCH = {
    "rowf": ("sbuf", [128, C * NF], "float32"),
    "rowb": ("sbuf", [128, C * NB], "bfloat16"),
    "tabf": ("sbuf", [128, 20 * NT], "float32"),
    "tabi": ("sbuf", [128, 20 * NI], "int32"),
    "tabu": ("sbuf", [128, 20 * NU], "uint16"),
    "fli": ("sbuf", [128, 20], "int32"),
    "mli": ("sbuf", [128, 20], "int32"),
    "jm": ("sbuf", [128, 2 * C], "float32"),
    "dcon": ("sbuf", [128, 2 * C], "bfloat16"),
    "pcol": ("sbuf", [128, 8], "int32"),
    "pcolf": ("sbuf", [128, 16], "float32"),
    "ui": ("sbuf", [128, 8], "int32"),
    "u16": ("sbuf", [128, 8], "uint16"),
    "half": ("sbuf", [128, 512], "bfloat16"),
    "et": ("sbuf", [128, 2048], "bfloat16"),
    "eq": ("sbuf", [128, 512], "float8_e4m3fn_x4"),
    "es": ("sbuf", [128, 512], "uint8"),
    "uin": ("sbuf", [128, 512], "bfloat16"),
    "vin": ("sbuf", [128, 512], "bfloat16"),
    "xin": ("sbuf", [128, 4 * C], "bfloat16"),
    "uq": ("sbuf", [128, 128], "float8_e4m3fn_x4"),
    "us": ("sbuf", [128, 128], "uint8"),
    "up": ("sbuf", [128, 128], "float8_e4m3fn_x4"),
    "ups": ("sbuf", [128, 128], "uint8"),
    "vq": ("sbuf", [128, 128], "float8_e4m3fn_x4"),
    "vs": ("sbuf", [128, 128], "uint8"),
    "wq": ("sbuf", [128, 512], "float8_e4m3fn_x4"),
    "wsc": ("sbuf", [128, 512], "uint8"),
    "ys": ("sbuf", [128, C], "float32"),
    "nls": ("sbuf", [128, C], "float32"),
    "ps": ("psum", [128, 512 * 8], "float32"),
}
for _r in range(ROUNDS + 1):
    SCRATCH["xq%d" % _r] = ("sbuf", [128, C], "float8_e4m3fn_x4")
    SCRATCH["xs%d" % _r] = ("sbuf", [128, C], "uint8")
for _r in range(ROUNDS):
    SCRATCH["lq%d" % _r] = ("sbuf", [128, C], "float8_e4m3fn_x4")
    SCRATCH["ls%d" % _r] = ("sbuf", [128, C], "uint8")
    SCRATCH["la%d" % _r] = ("sbuf", [128, 60], "uint16")
    SCRATCH["lb%d" % _r] = ("sbuf", [128, 20], "uint16")
    SCRATCH["sa%d" % _r] = ("sbuf", [128, 80], "uint16")
    SCRATCH["sb%d" % _r] = ("sbuf", [128, 20], "uint16")
for _h in range(2):
    for _k in ("fh", "fs", "gp", "zt", "xt"): SCRATCH["%s%d" % (_k, _h)] = ("sbuf", [128, 4 * C], "bfloat16")
    SCRATCH["rs%d" % _h] = ("sbuf", [128, 4 * C], "float32")
    SCRATCH["zq%d" % _h] = ("sbuf", [128, C], "float8_e4m3fn_x4")
    SCRATCH["zs%d" % _h] = ("sbuf", [128, C], "uint8")

LOADS = ("fl", "ml", "x", "u", "v", "wc", "ws")
STORES = ("oc", "os0", "os1", "os2", "os3", "y", "nl")
SEMAPHORES = ["ev", "es", "et", "eg", "rl"] + ["ld_" + n for n in LOADS] + ["st_" + n for n in STORES] \
    + ["%s%d" % (k, r) for k in ("aq", "aa", "ab") for r in range(ROUNDS)]

CY, GA, WAKE = 0.83 * 1.2, 1.5, 130.0
VB, LOOK, PW = 500.0, 150.0, 5.0
OFFS = "imdgjjbagglflfmjmjmjfhfbjgaggadgcabadamlfgfliaaefgcgfafhhmmgbhdgalbjdeadbmabldmfkmchgagjcmfmlajmamkmafmigcmdlihghblhcckekacmgeehjbiaahifjabajfgdagjmigacmiaakjmgfhjhjlihgcaagaaajbklmmifjadkelmgdgaagflhcimfajflmfmjedhdfgaimfmmhelghmjkhkmgemfkfgejeblmlkmfjhljlmmdmaaimfeigeccjmdlblcgjkbkhikhfgfafjbggfekaddhaamfgfegllajgaamgbmlfihiiaihgjklgmjhhhghgigaaaigajlckmakmammbadbgjkmkcliejmkcmeccbjaedjkkhffmjggcmjhadmikglamgkaahmfgmfbgaimaagjfkmmddafjgaecajbflhjelammlcmdeafjmlkjmhejdhbjikaddfajkgiiafdaadfbgfggflegkjeelmfgefeeffmccdbhbegkdbagmgekechddajdfmmahfmaddllhggblmmgegmamlecmhmehgljm"
FLEX = "----------------------------------------------------------------s-v---sv-----s---ss---------s---ss----s---s-s------------ss---------------sss--------------s--s--v------------------------s--s----------s---s--------------s--------------s---s-s---s---ss---ss----s---s----------------s-------------s---------------s------------v-----sv--s---v-------------------vs------------s---ss--ss--s-------v--s--s------s---s---sssss---ss---s-----s---s----ss---ss-----s------------------------------s------v-------s-vsv---v--s-------------------v-------------s---s----s--ss------s--s--s------------"


def add(P, cost, call, reads, writes, sem=None, val=16, after=(), lat=0.0):
    i = len(P["ops"])
    deps = set(after)
    for k in reads:
        if k in P["last"]: deps.add(P["last"][k])
    for k in writes:
        deps.update(P["readers"].get(k, []))
        if k in P["last"]: deps.add(P["last"][k])
    for k in reads: P["readers"].setdefault(k, []).append(i)
    for k in writes:
        P["last"][k] = i
        P["readers"][k] = []
    P["ops"].append({"c": cost, "f": call, "d": sorted(deps), "sem": sem, "val": val, "lat": lat})
    return i


def order(P):
    ops = P["ops"]
    n = len(ops)
    succ = [[] for _ in range(n)]
    for i in range(n):
        for j in ops[i]["d"]: succ[j].append(i)
    way = [0.0] * n
    for i in range(n - 1, -1, -1):
        best = 0.0
        for s in succ[i]: best = max(best, way[s] + WAKE)
        way[i] = best + min(ops[i]["c"].values()) + ops[i]["lat"]
    way = [x + 500.0 * (ord(OFFS[i]) - 103) if i < len(OFFS) else x for i, x in enumerate(way)]
    free = {"v": 0.0, "s": 0.0, "t": 0.0, "g": 0.0, "y": 0.0}
    done, seq = [0.0] * n, []
    left = [len(o["d"]) for o in ops]
    at = {}

    def open_(i):
        at[i] = max([done[j] + WAKE for j in ops[i]["d"]], default=0.0)
    for i in range(n):
        if left[i] == 0: open_(i)
    while at:
        cand = []
        for i, t in at.items():
            c = ops[i]["c"]
            if len(c) == 1:
                e = next(iter(c))
            elif i < len(FLEX) and FLEX[i] != "-":
                e = FLEX[i]
            else:
                tv = max(t, free["v"])
                busy = any(len(ops[j]["c"]) == 1 and "v" in ops[j]["c"] and u <= tv + c["v"] for j, u in at.items())
                e = "s" if max(t, free["s"]) + c["s"] <= tv + c["v"] + (VB if busy else 0.0) else "v"
            cand.append((t if e == "n" else max(t, free[e]), i, e))
        t0 = min(x[0] for x in cand)
        eng = max((x for x in cand if x[0] <= t0), key=lambda x: way[x[1]])[2]
        st, i, e = max((x for x in cand if x[2] == eng and x[0] <= t0 + LOOK), key=lambda x: way[x[1]] - PW * (x[0] - t0))
        del at[i]
        c = ops[i]["c"][e]
        if e != "n": free[e] = st + c
        done[i] = st + c + ops[i]["lat"]
        seq.append((st, i, e))
        for s in succ[i]:
            left[s] -= 1
            if left[s] == 0: open_(s)
    return seq, done


def emit(P, g, T, seq):
    ops = P["ops"]
    queue = {"v": g.vector, "s": g.scalar, "t": g.tensor, "g": g, "y": g.sync}
    name = {"v": "ev", "s": "es", "t": "et", "g": "eg"}
    count = {e: 0 for e in name}
    know = {e: {} for e in queue}
    clock, own = {}, {}
    for st, i, e in seq:
        o = ops[i]
        if e == "n":
            clock[i], own[i] = {o["sem"]: o["val"]}, (o["sem"], o["val"])
            continue
        want = {}
        for j in o["d"]:
            s, v = own[j]
            if v and know[e].get(s, 0) < v: want[s] = max(want.get(s, 0), v)
        for j in o["d"]:
            s, v = own[j]
            if want.get(s, 0) >= v > 0:
                for k, x in clock[j].items():
                    if k != s and k in want and want[k] <= x: del want[k]
        for s, v in want.items():
            queue[e].wait_ge(T.sem[s], v)
            know[e][s] = v
        for j in o["d"]:
            for k, x in clock[j].items(): know[e][k] = max(know[e].get(k, 0), x)
        ins = o["f"](e)
        clock[i] = dict(know[e])
        if o["sem"] is None:
            count[e] += 1
            own[i] = (name[e], count[e])
            ins.then_inc(T.sem[name[e]], 1)
        else:
            own[i] = (o["sem"], o["val"])
            if o["val"]: ins.then_inc(T.sem[o["sem"]], o["val"])
        if own[i][1]: clock[i][own[i][0]] = own[i][1]
    return count


def rank_program(g, core, T, topo):
    rank = T.rank_of(core)
    if rank is None: return
    P = {"ops": [], "last": {}, "readers": {}}
    slots = {"rowf": {}, "rowb": {}, "tabf": {}, "tabi": {}, "tabu": {}}
    top = {k: 0 for k in slots}

    def view(buf, unit, nm, w, a, b, s):
        d = slots[buf]
        if nm not in d:
            d[nm] = top[buf]
            top[buf] += (w + unit - 1) // unit * unit
        o = d[nm]
        b = w if b is None else b
        return T[buf][:, o + a:o + b:s] if s else T[buf][:, o + a:o + b]

    def F(nm, w=C, a=0, b=None, s=None): return view("rowf", C, nm, w, a, b, s)
    def B(nm, w=C, a=0, b=None, s=None): return view("rowb", C, nm, w, a, b, s)
    def tf(nm, w=20, a=0, b=None): return view("tabf", 20, nm, w, a, b, None)
    def ti(nm, w=20, a=0, b=None): return view("tabi", 20, nm, w, a, b, None)
    def tu(nm, w=20, a=0, b=None): return view("tabu", 20, nm, w, a, b, None)

    def ts(out, in0, s1, s2, op0, op1, rd, wr, n=20):
        def call(e): return g.vector.tensor_scalar(out, in0, s1, None, op0) if op1 is None else g.vector.tensor_scalar(out, in0, s1, s2, op0, op1)
        return add(P, {"v": max(60.0, n * CY)}, call, rd, wr)

    def tt(out, a, b, op, rd, wr, n=20, ind=False):
        return add(P, {"v": 55 + n * CY * GA if ind else max(60.0, 2 * n * CY)}, lambda e: g.vector.tensor_tensor(out, a, b, op), rd, wr)

    def scan(out, d0, d1, init, op0, op1, rd, wr, n=C, half=False):
        return add(P, {"v": n * CY * (0.5 if half else 1.0)}, lambda e: g.vector.tensor_tensor_scan(out, d0, d1, init, op0, op1), rd, wr)

    def vcopy(out, in_, rd, wr, n=20): return add(P, {"v": max(60.0, n * CY)}, lambda e: g.vector.tensor_copy(out, in_), rd, wr)

    def scatter(out, in_, rd, wr): return add(P, {"v": 1300.0}, lambda e: g.vector.tensor_copy(out, in_), rd, wr)

    def act(out, in_, func, rd, wr, scale=1.0, bias=None, ind=False):
        def call(e): return g.scalar.activation(out, in_, func, scale=scale) if bias is None else g.scalar.activation(out, in_, func, bias=bias, scale=scale)
        return add(P, {"s": 68 + C * CY * GA if ind else C * CY}, call, rd, wr)

    def either(call, rd, wr, ind, n=C): return add(P, {"v": 55 + n * CY * GA, "s": 68 + n * CY * GA} if ind else {"v": n * CY, "s": n * CY}, call, rd, wr)

    def move(out, in_, rd, wr, ind=False, scale=None):
        def call(e):
            if e == "s": return g.scalar.activation(out, in_, AF.Copy) if scale is None else g.scalar.activation(out, in_, AF.Copy, scale=scale)
            return g.vector.tensor_copy(out, in_) if scale is None else g.vector.tensor_scalar(out, in_, scale, None, A.mult)
        return either(call, rd, wr, ind)

    def affine(out, in_, a, b, rd, wr, ind=False):
        def call(e):
            if e == "s": return g.scalar.activation(out, in_, AF.Identity, bias=b, scale=a)
            return g.vector.tensor_scalar(out, in_, a, b, A.mult, A.add)
        return either(call, rd, wr, ind)

    def shift(out, in_, x, rd, wr):
        def call(e):
            if e == "s": return g.scalar.activation(out, in_, AF.Identity, bias=x)
            return g.vector.tensor_scalar(out, in_, x, None, A.add)
        return either(call, rd, wr, False)

    def quant(q, s, in_, n, rd, wr): return add(P, {"v": 12 + 0.22 * 4 * n * 1.2}, lambda e: g.vector.quantize_mx(q, s, in_), rd, wr)

    def bank(b): return T.ps[:, 512 * b:512 * b + C]

    def mm(b, w, ws, x, xs, rd):
        return add(P, {"t": 1.4 * 0.83 * (C + 16)}, lambda e: g.tensor.matmul_mx(bank(b), w, ws, x, xs, True, True), rd, ["ps%d" % b])

    def load(q, nm, out, in_):
        return add(P, {q: 60.0}, lambda e: (g.sync if e == "y" else g.scalar).dma_start(out, in_), [], [nm], sem="ld_" + nm, lat=2300.0)

    load("y", "fl", T.fli[:], T.fl[:, :])
    load("y", "ml", T.mli[:], T.ml[:, :])
    load("s", "x", T.xin[:], T.x[:, :])
    load("y", "u", T.uin[:], T.u[:, :])
    load("y", "wc", T.wq[:].bitcast(dt.uint8), T.wc[:, :])
    load("y", "ws", T.wsc[:], T.ws[:, :])
    load("y", "v", T.vin[:], T.v[:, :])

    def iota(out, pat, base, cm, wr, n, fl):
        def call(e): return g.iota(out, pat, base, cm, allow_small_or_imprecise_dtypes=True) if fl else g.iota(out, pat, base, cm)
        return add(P, {"g": 130 + 2 * n * CY}, call, [], wr)
    iota(T.pcol[:, 0:1], [[1, 1]], 0, 1, ["pcol"], 1, False)
    iota(F("iof"), [[1, C]], 0, 0, ["iof"], C, True)
    iota(T.jm[:], [[0, 40], [1, 16]], 0, 0, ["jm"], 2 * C, True)
    iota(T.ui[:], [[16, 8]], 0, 0, ["ui"], 8, False)
    ts(B("iob"), F("iof"), -float(MID), TINY, A.add, A.mult, ["iof"], ["iob"], C)
    pc, pf = T.pcol, T.pcolf
    for b in range(4):
        ts(pc[:, b + 1:b + 2], pc[:, 0:1], b, 1, A.logical_shift_right, A.bitwise_and, ["pcol"], ["pb%d" % b])
        ts(pf[:, b:b + 1], pc[:, b + 1:b + 2], 2.0 ** (STEPB << b) - 1, 1.0, A.mult, A.add, ["pb%d" % b], ["pf%d" % b])
    tt(pf[:, 4:5], pf[:, 0:1], pf[:, 1:2], A.mult, ["pf0", "pf1"], ["pf4"])
    ts(pf[:, 5:6], pf[:, 2:3], 2.0 ** (102 - 15 * STEPB), None, A.mult, None, ["pf2"], ["pf5"])
    tt(pf[:, 6:7], pf[:, 3:4], pf[:, 5:6], A.mult, ["pf3", "pf5"], ["pf6"])
    tt(pf[:, 7:8], pf[:, 4:5], pf[:, 6:7], A.mult, ["pf4", "pf6"], ["sc"])
    SC = pf[:, 7:8]
    ts(pc[:, 5:6], pc[:, 0:1], 15, None, A.bitwise_and, None, ["pcol"], ["p15"])
    vcopy(pf[:, 8:9], pc[:, 5:6], ["p15"], ["p15f"])
    ts(T.dcon[:], T.jm[:], pf[:, 8:9], 2.0 ** STEPB, A.is_gt, A.mult, ["jm", "p15f"], ["dcon"], 2 * C)
    ts(F("lab"), F("iof"), UNIT * TINY, -(MID + 1) * TINY, A.mult, A.add, ["iof"], ["lab"], C)
    ts(F("lab2"), F("iof"), UNIT * TINY, (UNIT - MID - 1) * TINY, A.mult, A.add, ["iof"], ["lab2"], C)
    for h in range(2):
        add(P, {"v": 300.0}, lambda e, h=h: g.vector.memset(F("gw%d" % h, 2 * C, 0, C + 8), 0.0), [], ["gw%d" % h])
        add(P, {"v": 150.0}, lambda e, h=h: g.vector.memset(B("eb%d" % h, 2 * C, 0, C + 16), -MID * TINY), [], ["eb%d" % h])
    add(P, {"v": 250.0}, lambda e: g.vector.memset(T.half[:], 0.5), [], ["half"])
    for b in range(4):
        add(P, {"g": 170 + 1024 * CY}, lambda e, b=b: g.affine_select(T.et[:, 512 * b:512 * b + 512], T.half[:], [[1, 512]], A.is_equal, 0.0, -b, -4),
            ["half"], ["et%d" % b])
        quant(T.eq[:, 128 * b:128 * b + 128], T.es[:, 128 * b:128 * b + 128], T.et[:, 512 * b:512 * b + 512], 128, ["et%d" % b], ["eq%d" % b])

    quant(T.xq0[:], T.xs0[:], T.xin[:], C, ["x"], ["X0"])
    vcopy(T.u16[:], T.ui[:], ["ui"], ["u16"])
    quant(T.uq[:], T.us[:], T.uin[:], 128, ["u"], ["uq"])
    add(P, {"v": 250.0}, lambda e: g.vector.tensor_copy(T.up[:].bitcast(dt.uint32), T.uq[:].bitcast(dt.uint32).indirect(T.u16[:])), ["uq", "u16"], ["up"])
    add(P, {"v": 250.0}, lambda e: g.vector.tensor_copy(T.ups[:], T.us[:].indirect(T.u16[:])), ["uq", "u16"], ["ups"])
    quant(T.vq[:], T.vs[:], T.vin[:], 128, ["v"], ["vq"])

    def compact(out, nm, bias, rd, wr, w=1):
        n = w * C
        scan(B(nm + "k", n), T.dcon[:, 0:n], B(nm, n), 0.0, A.mult, A.add, rd + ["dcon"], [nm + "k"], n, True)
        if out is not None: ts(out, B(nm + "k", n, 15, n, 16), SC, bias, A.mult, A.add, [nm + "k", "sc"], wr, 20 * w)

    vcopy(tu("LG0", 40, 0, 20), T.fli[:], ["fl"], ["L0_0"])
    vcopy(tu("M16"), T.mli[:], ["ml"], ["M16"])
    scatter(B("gl0").indirect(tu("LG0", 40, 0, 20)), B("iob"), ["L0_0", "iob"], ["gl0"])
    compact(tu("LG0", 40, 20, 40), "gl0", MID + 0.25, ["gl0"], ["GL_0"])
    move(B("mr"), B("iob").indirect(tu("M16")), ["iob", "M16"], ["mr"], ind=True)
    tt(F("sgd"), B("mr"), B("iob"), A.subtract, ["mr", "iob"], ["sgd"], C)
    act(F("sg"), F("sgd"), AF.Sign, ["sgd"], ["sg"], scale=2.0 ** 97)

    sent = [0]
    peers = [T.cores[rank ^ m] for m in MASKS]
    common = [e for e in topo.engines(core, peers[0]) if all(e in topo.engines(core, p) and e in topo.engines(p, core) for p in peers)]
    for r in range(ROUNDS):
        h = r % 2
        R = lambda nm: "%s_%d" % (nm, h)
        partner = T.cores[rank ^ MASKS[r]]
        rid, pid, _s = topo.addr(partner)
        msk, ne = sum(1 << e for e in common), len(common)
        X, Xq, Xs = "X%d" % r, T["xq%d" % r], T["xs%d" % r]

        def send(sem, pieces, rd, key, lat):
            for dst, src in pieces:
                last = add(P, {"g": 300.0}, lambda e, dst=dst, src=src, sem=sem, rid=rid, pid=pid, msk=msk: g.remote_dma(dst, src, T.sem[sem], T.sem.rl, pid, rid, msk),
                           rd, ["net"], sem="rl", val=0)
                sent[0] += ne
            add(P, {"n": 0.0}, None, [], [key], sem=sem, val=ne * len(pieces), after=[last], lat=lat)

        send("aq%d" % r, [(T["lq%d" % r][:].bitcast(dt.uint8), Xq[:].bitcast(dt.uint8)), (T["ls%d" % r][:], Xs[:])], [X], "Y%d" % r, 9000.0)

        mm(0, T.up[:], T.ups[:], Xq[:], Xs[:], ["up", "ups", X])
        move(F(R("s")), bank(0), ["ps0"], [R("s")])
        for b in range(4):
            mm(1 + b, T.eq[:, 128 * b:128 * b + 128], T.es[:, 128 * b:128 * b + 128], Xq[:], Xs[:], ["eq%d" % b, X])
            move(T["fh%d" % h][:, C * b:C * b + C], bank(1 + b), ["ps%d" % (1 + b)], ["fh%d%d" % (h, b)])

        LG, LN = "LG%d" % r, "LG%d" % (r + 1)
        FL, GL, FN, GN = "L0_%d" % r, "GL_%d" % r, "L0_%d" % (r + 1), "GL_%d" % (r + 1)
        fl_, gl_, fn_, gn_ = tu(LG, 40, 0, 20), tu(LG, 40, 20, 40), tu(LN, 40, 0, 20), tu(LN, 40, 20, 40)
        L = [FL] + [R("L%d" % k) for k in range(1, 8)]
        lists = [fl_] + [tu(k) for k in L[1:]]
        move(B(R("fr0")), B("iob").indirect(fl_), ["iob", FL], [R("fr0")], ind=True)
        for nm, x in (("key0", 0.0), ("w0", 1.0)):
            affine(F(R(nm)), B("iob").indirect(fl_), UNIT, (UNIT * MID - MID + x) * TINY, ["iob", FL], [R(nm)], ind=True)
        for k in range(9):
            if k < 7:
                nx = R("fr%d" % (k + 1))
                move(B(nx), B(R("fr%d" % k)).indirect(lists[k]), [R("fr%d" % k), L[k]], [nx], ind=True)
                compact(lists[k + 1], nx, MID + 0.25, [nx], [L[k + 1]])
            q = k if k < 8 else 6
            a, b = R("key%d" % (k % 2)), R("key%d" % ((k + 1) % 2))
            w, wn = R("w%d" % (k % 2)), R("w%d" % ((k + 1) % 2))
            tt(F(b), F(w).indirect(lists[q]), F(a), A.min, [w, L[q], a], [b], C, True)
            if k < 8: shift(F(wn), F(b), (2.0 ** (k + 1) if k < 7 else 64.0) * TINY, [b], [wn])
        key = R("key1")

        act(B(R("kb")), F(key), AF.Identity, [key], [R("kb")], scale=1 / UNIT, bias=-MID * TINY)
        RL = R("RL")
        compact(tu(RL, 40, 0, 20), R("kb"), MID + 0.25, [R("kb")], [RL + "a"])
        ts(tu(RL, 40, 20, 40), B(R("kb") + "k", C, 15, C, 16), SC, MID + 1.25, A.mult, A.add, [R("kb") + "k", "sc"], [RL + "b"])
        tt(F(R("mx")), F(key), F("lab"), A.max, [key, "lab"], [R("mx")], C)
        eb, be = "eb%d" % h, R("be")
        scan(B(eb, 2 * C, 1, C + 1), F(R("mx")), F("lab"), -MID * TINY, A.add, A.subtract, [R("mx"), "lab"], [eb])
        gw, prow = "gw%d" % h, R("prow")
        scan(F(gw, 2 * C, 1, C + 1), F(R("mx")), F("lab2"), 0.0, A.add, A.subtract, [R("mx"), "lab2"], [gw])
        tt(B(prow), F(gw, 2 * C, 0, C + 1).indirect(tu(RL, 40, 0, 20)), F(key), A.add, [gw, RL + "a", key], [prow], C, True)
        compact(tu(R("P16")), prow, MID + 0.25, [prow], [R("P16")])
        ts(ti(R("pos")), B(prow + "k", C, 15, C, 16), SC, float(MID), A.mult, A.add, [prow + "k", "sc"], [R("pos")])
        it = R("it")
        move(B(be, 2 * C, 0, C), B(eb, 2 * C, 0, C + 1).indirect(tu(RL, 40, 0, 20)), [eb, RL + "a"], [be + "b"], ind=True)
        affine(B(be, 2 * C, C, 2 * C), B(eb, 2 * C, 0, C + 1).indirect(tu(RL, 40, 20, 40)), 1.0, -TINY, [eb, RL + "b"], [be + "e"], ind=True)
        compact(ti(it, 80, 40, 80), be, float(MID), [be + "b", be + "e"], [it + "b"], 2)
        tt(ti(it, 80, 20, 40), ti(R("pos")), ti(it, 80, 40, 60), A.subtract, [R("pos"), it + "b"], [it + "c"])
        tt(ti(it, 80, 0, 20), ti(it, 80, 60, 80), ti(it, 80, 40, 60), A.subtract, [it + "b"], [it + "n"])
        sa, sb, SA, O16 = T["sa%d" % r], T["sb%d" % r], "sa%d" % r, "sb%d" % r
        vcopy(sa[:], ti(it, 80), [it + "n", it + "c", it + "b"], [SA], 80)
        E16 = sa[:, 60:80]
        send("aa%d" % r, [(T["la%d" % r][:], sa[:, 0:60])], [SA], "la%d" % r, 4500.0)
        ts(tf(R("nf")), ti(it, 80, 0, 20), 1.0, None, A.add, None, [it + "n"], [R("nf")])
        ol = R("ol")
        scatter(B(ol).indirect(tu(R("P16"))), B("iob"), [R("P16"), "iob"], [ol])
        compact(sb[:], ol, MID + 0.25, [ol], [O16])
        send("ab%d" % r, [(T["lb%d" % r][:], sb[:])], [O16], "lb%d" % r, 4500.0)
        act(B(R("flag")), B("iob").indirect(sa[:, 20:40]), AF.Relu, ["iob", SA], [R("flag")], scale=-2.0 ** 97, bias=(1.0 - MID) * TINY * 2.0 ** 97, ind=True)
        act(B(R("d0")), B(R("flag")).indirect(sb[:]), AF.Copy, [R("flag"), O16], [R("d0")], scale=-2.0 ** 97, ind=True)
        move(B(R("d1")), B(R("d0")), [R("d0")], [R("d1")], scale=-1.0)
        fg = R("fg")
        move(B(fg, 2 * C, 0, C), B(R("fr0")).indirect(tu("M16")), [R("fr0"), "M16"], [fg + "f"], ind=True)
        move(B(fg, 2 * C, C, 2 * C), B("mr").indirect(gl_), ["mr", GL], [fg + "g"], ind=True)
        compact(tf(R("fgv"), 40), fg, MID + 0.25, [fg + "f", fg + "g"], [R("fgv")], 2)
        ts(tf(R("fg0"), 40), tu(LG, 40), 0.25, None, A.add, None, [FL, GL], [R("fg0")], 40)
        tt(tf(R("fgd"), 40), tf(R("fgv"), 40), tf(R("fg0"), 40), A.subtract, [R("fgv"), R("fg0")], [R("fgd")], 40)
        ts(tf(R("fgs"), 40), tf(R("fgd"), 40), SC, None, A.mult, None, [R("fgd"), "sc"], [R("fgs")], 40)

        move(F(R("so")), F(R("s")).indirect(sb[:]), [R("s"), O16], [R("so")], ind=True)
        scan(F(R("pm")), B(R("d0")), F(R("so")), -2.0 ** 92, A.add, A.max, [R("d0"), R("so")], [R("pm")])
        tt(F(R("eq")), F(R("pm")).indirect(E16), F(R("s")), A.subtract, [R("pm"), SA, R("s")], [R("eq")], C, True)
        tt(B(R("cd")), F(R("eq")).indirect(sb[:]), B(ol), A.add, [R("eq"), O16, ol], [R("cd")], C, True)
        scan(B(R("cs")), B(R("d1")), B(R("cd")), 0.0, A.add, A.min, [R("d1"), R("cd")], [R("cs")], C, True)
        move(B(R("gk")), B(R("cs")).indirect(E16), [R("cs"), SA], [R("gk")], ind=True)
        l16 = R("l16")
        compact(tu(l16), R("gk"), MID + 0.25, [R("gk")], [l16])

        xa = R("xa")
        for q in range(3):
            move(B(xa, 3 * C, C * q, C * q + C), B("iob").indirect(T["la%d" % r][:, 20 * q:20 * q + 20]), ["iob", "la%d" % r], [xa + str(q)], ind=True)
        move(B(R("oe")), B("iob").indirect(T["lb%d" % r][:]), ["iob", "lb%d" % r], [R("oe")], ind=True)
        move(B(R("xn")), B(xa, 3 * C, 0, C).indirect(tu(l16)), [xa + "0", l16], [R("xn")], ind=True)
        compact(ti(R("xni")), R("xn"), MID + 1.0, [R("xn")], [R("xni")])
        xd = R("xd")
        for q in (1, 2): move(B(xd, 2 * C, C * q - C, C * q), B(xa, 3 * C, C * q, C * q + C).indirect(tu(l16)), [xa + str(q), l16], [xd + str(q)], ind=True)
        compact(None, xd, 0.0, [xd + "1", xd + "2"], None, 2)
        ts(tf(R("xb")), B(xd + "k", 2 * C, C + 15, 2 * C, 16), SC, float(MID), A.mult, A.add, [xd + "k", "sc"], [R("xb")])
        move(B(R("xp")), B(R("prow")).indirect(tu(l16)), [R("prow"), l16], [R("xp")], ind=True)
        compact(None, R("xp"), 0.0, [R("xp")], None)
        tt(tf(R("dl")), B(R("xp") + "k", C, 15, C, 16), B(prow + "k", C, 15, C, 16), A.subtract, [R("xp") + "k", prow + "k"], [R("dl")])
        ts(tf(R("ng")), tf(R("dl")), SC, -0.5, A.mult, A.is_lt, [R("dl"), "sc"], [R("ng")])
        tt(tf(R("nn")), tf(R("ng")), tf(R("nf")), A.mult, [R("ng"), R("nf")], [R("nn")])
        vcopy(tf(R("ne")), ti(R("xni")), [R("xni")], [R("ne")])
        add(P, {"v": 300.0}, lambda e, a=R("rn"), b=R("ne"): g.vector.reciprocal(tf(a), tf(b)), [R("ne")], [R("rn")])
        tt(tf(R("zr")), B(xd + "k", 2 * C, 15, C, 16), tf(R("dl")), A.subtract, [xd + "k", R("dl")], [R("zr")])
        ts(tf(R("z0")), tf(R("zr")), SC, MID + 0.5, A.mult, A.add, [R("zr"), "sc"], [R("z0")])
        tt(tf(R("zh")), tf(R("z0")), tf(R("nn")), A.subtract, [R("z0"), R("nn")], [R("zh")])
        tt(tf(R("tq")), tf(R("zh")), tf(R("rn")), A.mult, [R("zh"), R("rn")], [R("tq")])
        ts(ti(R("qi")), tf(R("tq")), -0.5, None, A.add, None, [R("tq")], [R("qi")])
        tt(tf(R("zb")), tf(R("zh")), tf(R("xb")), A.add, [R("zh"), R("xb")], [R("zb")])
        tt(tf(R("m1")), ti(R("qi")), tf(R("ne")), A.mult, [R("qi"), R("ne")], [R("m1")])
        tt(tf(R("pp")), tf(R("zb")), tf(R("m1")), A.subtract, [R("zb"), R("m1")], [R("pp")])
        ts(tu(R("PL")), tf(R("pp")), -0.25, None, A.add, None, [R("pp")], [R("PL")])
        move(B(R("tr")), B(R("oe")).indirect(tu(R("PL"))), [R("oe"), R("PL")], [R("tr")], ind=True)
        T16 = R("T16")
        compact(tu(T16), R("tr"), MID + 0.25, [R("tr")], [T16])

        tt(F(R("st")), F(R("s")).indirect(tu(T16)), F("sg"), A.mult, [R("s"), T16, "sg"], [R("st")], C, True)
        for c in range(2):
            a, b = C // 2 * c, C // 2 * c + C // 2
            either(lambda e, o=F(R("su"), C, a, b), i=F(R("st"), C, a, b): g.vector.tensor_copy(o, i) if e == "v" else g.scalar.activation(o, i, AF.Copy),
                   [R("st")], [R("su") + "ab"[c]], False, C // 2)
        tt(F(R("sv")), F(R("st")).indirect(tu("M16")), F(R("su")), A.add, [R("st"), R("su") + "a", R("su") + "b", "M16"], [R("sv")], C, True)
        ts(B(R("sw")), F(R("sv")), 0.0, TINY, A.is_lt, A.mult, [R("sv")], [R("sw")], C)
        move(B(R("swg")), B(R("sw")).indirect(gl_), [R("sw"), GL], [R("swg")], ind=True)
        for nm, a, out, kk in (("sw", 0, fn_, FN), ("swg", 20, gn_, GN)):
            compact(None, R(nm), 0.0, [R(nm)], None)
            tt(tf(R(nm + "x")), B(R(nm) + "k", C, 15, C, 16), tf(R("fgs"), 40, a, a + 20), A.mult, [R(nm) + "k", R("fgs")], [R(nm + "x")])
            tt(tf(R(nm + "y")), tf(R(nm + "x")), tf(R("fg0"), 40, a, a + 20), A.add, [R(nm + "x"), R("fg0")], [R(nm + "y")])
            vcopy(out, tf(R(nm + "y")), [R(nm + "y")], [kk])

        fh, fs, gp, zt, xt, rs = [T["%s%d" % (k, h)] for k in ("fh", "fs", "gp", "zt", "xt", "rs")]
        for b in range(4):
            bk, c = (5, 6, 7, 0)[b], slice(C * b, C * b + C)
            mm(bk, T.eq[:, 128 * b:128 * b + 128], T.es[:, 128 * b:128 * b + 128], T["lq%d" % r][:], T["ls%d" % r][:], ["eq%d" % b, "Y%d" % r])
            move(fs[:, c], bank(bk), ["ps%d" % bk], ["fs%d%d" % (h, b)])
            move(gp[:, c], fs[:, c].indirect(tu(T16)), ["fs%d%d" % (h, b), T16], ["gp%d%d" % (h, b)], ind=True)
            tt(zt[:, b:4 * C:4], fh[:, c].indirect(fn_), gp[:, c], A.add, ["fh%d%d" % (h, b), FN, "gp%d%d" % (h, b)], ["zt%d%d" % (h, b)], C, True)
        zq, zs = T["zq%d" % h], T["zs%d" % h]
        quant(zq[:], zs[:], zt[:], C, ["zt%d%d" % (h, b) for b in range(4)], ["zq%d" % h])
        for b in range(4):
            c = slice(C * b, C * b + C)
            mm(1 + b, T.wq[:, 128 * b:128 * b + 128], T.wsc[:, 128 * b:128 * b + 128], zq[:], zs[:], ["wc", "ws", "zq%d" % h])
            move(rs[:, c], bank(1 + b), ["ps%d" % (1 + b)], ["rs%d%d" % (h, b)], scale=2.0 ** -6)
            tt(xt[:, b:4 * C:4], rs[:, c].indirect(gn_), fh[:, c], A.add, ["rs%d%d" % (h, b), GN, "fh%d%d" % (h, b)], ["xt%d%d" % (h, b)], C, True)
        quant(T["xq%d" % (r + 1)][:], T["xs%d" % (r + 1)][:], xt[:], C, ["xt%d%d" % (h, b) for b in range(4)], ["X%d" % (r + 1)])

    q, s, X = T["xq%d" % ROUNDS], T["xs%d" % ROUNDS], "X%d" % ROUNDS

    def store(nm, out, in_, rd): add(P, {"y": 60.0}, lambda e: g.sync.dma_start(out, in_), rd, [], sem="st_" + nm, lat=2000.0)
    act(T.nls[:], F("iof").indirect(tu("LG%d" % ROUNDS, 40, 0, 20)), AF.Copy, ["iof", "L0_%d" % ROUNDS], ["nls"], ind=True)
    store("nl", T.nl[:, :], T.nls[0:128:16, :], ["nls"])
    mm(1, T.vq[:], T.vs[:], q[:], s[:], ["vq", X])
    move(T.ys[:], bank(1), ["ps1"], ["ys"])
    store("oc", T.oc[:, :], q[:].bitcast(dt.uint8), [X])
    for k in range(4): store("os%d" % k, T.osc[4 * k:4 * k + 4, :], s[32 * k:32 * k + 4, :], [X])
    store("y", T.y[:, :], T.ys[:], ["ys"])

    seq, done = order(P)
    count = emit(P, g, T, seq)
    for nm in STORES: g.sync.wait_ge(T.sem["st_" + nm], 16)
    g.wait_ge(T.sem.rl, sent[0])
    for e, nm in (("v", "ev"), ("s", "es"), ("t", "et"), ("g", "eg")): g.sync.wait_ge(T.sem[nm], count[e])
